import numpy as np, ml_dtypes
CORES = [5,29,101,125,133,157,229,253]
N = 8
BF = ml_dtypes.bfloat16
D, L, H, S1, S2, VI = 1760, 128, 64, 4, 1, 4
def effects(rng):
    cap = rng.integers(1, 256, (N, 8, 1, D))
    return np.minimum((rng.random((N, 8, 16, D)) * (cap + 1)).astype(np.int64), cap)
def near(rng, n, share, few=64):
    pop = rng.integers(0, D, (N, 8, few)); v = rng.integers(0, D, (N, 8, 16, n))
    c = np.take_along_axis(pop, rng.integers(0, few, (N, 8, 16 * n)), 2).reshape(N, 8, 16, n)
    return np.where(rng.random(v.shape) < share, c, v)
def rows(rng, n):
    return np.argsort(np.argsort(rng.random((N, 8, 16, L)), axis=2), axis=2) < n
def forest(rng, filled, own, deep):
    o = np.argsort(np.where(filled, rng.random(filled.shape), 2.0), axis=2); r = np.arange(16)[:, None]
    u = rng.random(filled.shape); b = np.minimum((rng.random(filled.shape) * (r + 1)).astype(np.int64), r)
    b = np.where(u < own, r, np.where(u > 1 - deep, np.maximum(r - 1, 0), b))
    w = np.zeros(filled.shape, np.int64); np.put_along_axis(w, o, np.take_along_axis(o, b, 2), 2)
    return np.where(filled, w, 0)
def pack(eff, rem, lim, drugs, why, filled):
    return {"eff": np.ascontiguousarray(eff.reshape(N, 128, D)).astype(np.float32).astype(BF), "rem": np.ascontiguousarray(rem.reshape(N, 128, D)).astype(np.int32),
            "lim": np.repeat(lim, 16, axis=1)[:, :, None].astype(np.int32), "drugs": np.ascontiguousarray(np.where(filled, drugs, D).reshape(N, 128, L)).astype(np.int32),
            "why": np.ascontiguousarray(np.where(filled, why, 0).reshape(N, 128, L)).astype(np.int32)}
def setup_inputs(rng):
    n = np.maximum(rng.integers(0, 17, (N, 8, 1, L)), rng.integers(0, 17, (N, 8, 1, L)))
    filled = rows(rng, n); why = forest(rng, filled, 0.3, 0.3)
    return pack(effects(rng), near(rng, D, 0.3), rng.integers(6000, 20000, (N, 8)), near(rng, L, 0.3), why, filled)
def setup_inputs_ties(rng):
    v = rng.integers(0, 256, (N, 8, 16)); v[:, :, 0] = 255
    sh = rng.integers(0, 16, (N, 8, 1, D)); sh[:, ::2, :, 1::2] = sh[:, ::2, :, ::2] + 8
    ix = (np.arange(16)[:, None] + sh) % 16
    eff = np.take_along_axis(v, ix.reshape(N, 8, 16 * D), 2).reshape(N, 8, 16, D)
    lim = np.minimum(rng.integers(3, 12, (N, 8)) * np.add.reduce(v, axis=2), 65280)
    filled = rows(rng, rng.integers(1, 17, (N, 8, 1, L))); drugs = near(rng, L, 0.9, 6)
    pair = rng.random((N, 8, 1, L)) < 0.5; pair[:, 1::2] = False
    twin = np.repeat(drugs[:, :, ::2], 2, axis=2); twin[:, :, 1::2] = twin[:, :, 1::2] ^ 1
    drugs = np.where(pair, twin, drugs); filled = np.where(pair, np.repeat(filled[:, :, ::2], 2, axis=2), filled)
    why = forest(rng, filled, 0.4, 0.2)
    return pack(eff, near(rng, D, 0.7, 6), lim, drugs, why, filled)
def setup_inputs_corners(rng):
    eff = effects(rng); eff[..., 0] = 0; eff[..., D - 1] = 255
    lim = rng.choice(np.array([1, 12000, 65280]), (N, 8)); lim[:, 1] = 1; lim[:, 2] = 65280
    kind = rng.integers(0, 10, (N, 8, 1, L)); m = np.arange(16)[:, None]; hv = rng.random((N, 8, 1, L)) < 0.5
    filled = rows(rng, np.where(kind == 6, 15, rng.integers(0, 17, (N, 8, 1, L))))
    filled = filled | (kind == 1) | (kind == 2) | (kind == 5) | (kind == 8) | (kind == 9)
    filled = np.where(kind == 0, False, np.where(kind == 3, m == 15, np.where(kind == 4, m == 0, filled)))
    why = forest(rng, filled, 0.2, 0.2)
    for k, w in ((1, np.maximum(m - 1, 0)), (2, m), (5, 0 * m), (8, np.minimum(m + 1, 15)), (9, 0 * m + 15)):
        why = np.where(kind == k, w, why)
    drugs = near(rng, L, 0.3)
    low = (kind == 1) | (kind == 5); high = (kind == 8) | (kind == 9)
    top = (low & (m == np.where(hv, 0, 15))) | (high & (m == np.where(hv, 15, 0)))
    drugs = np.where(top | (kind == 3), D - 1, np.where(kind == 4, 0, drugs))
    return pack(eff, near(rng, D, 0.3), lim, drugs, why, filled)
def setup_inputs_great(rng):
    low = np.array([11, 0, 1, 0, 11, 0, 0, 11]).reshape(8, 1, 1); lane = np.arange(L)
    eff = effects(rng); rem = near(rng, D, 0.3); drugs = near(rng, L, 0.3); lim = rng.integers(6000, 20000, (N, 8))
    filled = rows(rng, rng.integers(low, 16, (N, 8, 1, L)))
    for g in (1, 6):
        eff[:, g] = rng.integers(0, 16, (N, 16, D)) < np.array([0, 1, 2, 4, 6, 8, 12, 16])[np.arange(D) % 8]
        lim[:, g] = 1
        h = np.maximum(rng.integers(-4, 8, (N, 1, L)), 0); pure = rng.random((N, 1, L)) < 0.6
        drugs[:, g] = np.where(pure, drugs[:, g] // 8 * 8 + h, drugs[:, g])
        filled[:, g] = filled[:, g] | (pure & (h == 0))
        faint = rng.random((N, 1, D)) < 0.3
        rem[:, g] = np.where(faint, rem[:, g] // 8 * 8 + rng.integers(0, 2, (N, 16, D)), rem[:, g])
    eff[:, 2] = rng.integers(0, 101, (N, 16, D)); lim[:, 2] = 1
    for q in range(N):
        o = rng.permutation(D); i = rng.integers(0, 16, L)
        eff[q, 2][:, o[:L]] = rng.integers(128, 256, (16, L))
        v = rng.choice(o[L:], (16, L)); v[i, lane] = o[:L]; drugs[q, 2] = v
        filled[q, 2][i, lane] = True
    for g in (0, 4, 7):
        eff[:, g] = rng.integers(0, 32, (N, 16, D)) + rng.integers(192, 225, (N, 1, 1))
        if g == 7:
            eff[:, g, :, 7::8] = 255
            drugs[:, g, :, L - 1] = drugs[:, g, :, L - 1] // 8 * 8 + 7
            filled[:, g, :, L - 1] = np.arange(16)[None, :] != rng.integers(0, 16, (N, 1))
        e = np.add.reduce(eff[:, g], axis=1)
        b = np.add.reduce(np.where(filled[:, g], np.take_along_axis(e, drugs[:, g].reshape(N, 16 * L), 1).reshape(N, 16, L), 0), axis=1)
        i = np.argmax(rng.random((N, L)) * (b % 128 > 0), axis=1); v = b[np.arange(N), i]
        lim[:, g] = v + (v % 256 > 128)
    lim[N - 1, 7] = 61200
    filled[0] = True; filled[2] = True
    o = rng.permutation(8 * L)[:int(rng.integers(100, 201))]
    for j in o: filled[2, j // L, :, j % L] = False
    return pack(eff, rem, lim, drugs, forest(rng, filled, 0.3, 0.3), filled)
def setup_inputs_spread(rng):
    cap = np.exp2(8 * rng.random((N, 8, 1, D))).astype(np.int64); cap = np.minimum(cap, 255)
    eff = np.minimum((rng.random((N, 8, 16, D)) * (cap + 1)).astype(np.int64), cap)
    e = rng.choice(np.array([1.0, 3.0, 8.0]), (N, 8, 1, 1))
    rem = np.minimum((D * rng.random((N, 8, 16, D)) ** 3).astype(np.int64), D - 1); drugs = np.minimum((D * rng.random((N, 8, 16, L)) ** e).astype(np.int64), D - 1)
    lim = np.minimum(np.maximum(np.exp2(16 * rng.random((N, 8))).astype(np.int64), 1), 65280); lim[:, 5] = rng.integers(3000, 9000, N)
    filled = rows(rng, rng.integers(0, 17, (N, 8, 1, L))); why = forest(rng, filled, rng.random((N, 8, 1, L)), 0.3)
    return pack(eff, rem, lim, drugs, why, filled)
def setup_inputs_ends(rng):
    eff = 255 * (rng.random((N, 8, 16, D)) < rng.choice(np.array([0.0, 0.5, 1.0]), (N, 8, 1, D))).astype(np.int64)
    case = rng.integers(0, 4, (N, 8)); case[0, 0] = 1; case[N - 1, 7] = 0; case[:, 4] = 2
    a = np.where((case == 0) | (case == 3), 255, np.where(case == 1, 0, -1))[:, :, None]; b = np.where(case == 0, 255, np.where((case == 1) | (case == 3), 0, -1))[:, :, None]
    eff[..., 0] = np.where(a >= 0, a, eff[..., 0]); eff[..., D - 1] = np.where(b >= 0, b, eff[..., D - 1])
    rem = (D - 1) * rng.integers(0, 2, (N, 8, 16, D))
    lim = np.where(rng.random((N, 8)) < 0.5, 1, 65280); lim[:, 0] = 1; lim[:, 7] = 65280
    filled = rng.random((N, 8, 16, L)) < 0.65; filled[:, :, 0] = True; filled[:, :, 15] = True
    none = rng.random((N, 8, 1, L)) < 0.05; full = rng.random((N, 8, 1, L)) < 0.1; full[..., 1] = True; full[..., L - 1] = True
    filled = full | (filled & ~none)
    drugs = np.where(rng.random((N, 8, 16, L)) < 0.7, 0, D - 1); drugs[..., 1] = 0; drugs[..., L - 1] = D - 1
    why = 15 * rng.integers(0, 2, (N, 8, 16, L)); z = rng.integers(0, 2, (N, 8, L))
    why[:, :, 0] = 15 * z; why[:, :, 15] = np.where(z == 1, 15, why[:, :, 15])
    return pack(eff, rem, lim, drugs, why, filled)
def check_inputs(d):
    bad = []
    for k, lo, hi in (("eff", 0, 255), ("rem", 0, D - 1), ("lim", 1, 65280), ("drugs", 0, D), ("why", 0, 15)):
        v = np.asarray(d[k]).astype(np.float64)
        if not (np.min(v) >= lo and np.max(v) <= hi): bad.append("range of " + k)
        elif k == "eff" and np.any(v != np.floor(v)): bad.append("whole numbers in eff")
    v = np.asarray(d["lim"]).reshape(N, 8, 16)
    if np.any(v != v[:, :, :1]): bad.append("lim alike in a group")
    if "range of drugs" in bad or "range of why" in bad: return bad
    filled = np.asarray(d["drugs"]).reshape(N, 8, 16, L) < D; w = np.asarray(d["why"]).astype(np.int64).reshape(N, 8, 16, L)
    if np.any(~filled & (w != 0)): bad.append("why is 0 in empty rows")
    if np.any(filled & ~np.take_along_axis(filled, w, 2)): bad.append("reasons are filled rows")
    c = w
    for _ in range(4): c = np.take_along_axis(c, c, 2)
    if np.any(filled & (np.take_along_axis(w, c, 2) != c)): bad.append("reasons end in a row that is its own reason")
    return bad
def stand(A, a, t):
    return np.concatenate([A[(a - S1 * t) % N][..., :H], A[(a - S2 * t) % N][..., H:]], axis=2)
def reference(eff, rem, lim, drugs, why):
    X = eff.astype(np.float32).astype(np.int32).reshape(N, 8, 16, D)
    X = np.concatenate([X, np.zeros((N, 8, 16, 1), np.int32)], axis=3)
    R = rem.astype(np.int64).reshape(N, 8, 16, D); B = lim.astype(np.int64).reshape(N, 8, 16)[:, :, :1]
    P = drugs.astype(np.int64).reshape(N, 8, 16, L); Q = why.astype(np.int64).reshape(N, 8, 16, L)
    m16 = np.arange(16)[None, :, None]; c = np.zeros(N, np.int64)
    for t in range(VI):
        NP = np.zeros_like(P); NQ = np.zeros_like(Q); stops = np.zeros(N, np.int64)
        for a in range(N):
            p = stand(P, a, t); w = stand(Q, a, t); filled = p < D
            x = np.take_along_axis(X[a], p.reshape(8, 1, 16 * L), 2).reshape(8, 16, 16, L)
            T = np.add.reduce(x, axis=2); burden = np.add.reduce(T, axis=1)
            stop = np.any(filled, axis=1) & ((burden >= B[a] + c[a]) | np.all(filled, axis=1))
            s = np.argmax(np.where(filled, np.add.reduce(x, axis=1), -1), axis=1)[:, None, :]
            cur = np.broadcast_to(m16, p.shape); reach = np.zeros(p.shape, bool)
            for _ in range(16):
                reach = reach | (cur == s); cur = np.take_along_axis(w, cur, 1)
            gone = reach & filled & stop[:, None, :]
            d = np.take_along_axis(p, s, 1)[:, 0]; xs = np.take_along_axis(x, s[:, None], 2)[:, :, 0]; xn = (xs + (T >> 4)) >> 1
            p = np.where(gone, D, p); w = np.where(gone, 0, w); filled = p < D; some = np.any(filled, axis=1)
            U = np.add.reduce(np.where(filled[:, None], x, 0), axis=2)
            f = np.argmax(U, axis=1)
            k = np.argmax(np.where(filled, np.take_along_axis(x, f[:, None, None, :], 1)[:, 0], -1), axis=1)
            dk = np.minimum(np.take_along_axis(p, k[:, None, :], 1), D - 1)
            cand = np.take_along_axis(R[a], dk, 2)
            xc = np.take_along_axis(X[a], cand.reshape(8, 1, 16 * L), 2).reshape(8, 16, 16, L)
            score = np.add.reduce(np.abs(255 - xc - (U >> 4)[:, :, None, :]), axis=1)
            new = np.take_along_axis(cand, np.argmin(score, axis=1)[:, None, :], 1)
            put = (m16 == np.argmin(filled, axis=1)[:, None, :]) & some[:, None, :]
            p = np.where(put, new, p); w = np.where(put, k[:, None, :], w)
            for A, v in ((NP, p), (NQ, w)):
                A[(a - S1 * t) % N, :, :, :H] = v[..., :H]; A[(a - S2 * t) % N, :, :, H:] = v[..., H:]
            for g in range(8):
                lanes = np.flatnonzero(stop[g]); u, i = np.unique(d[g, lanes], return_index=True)
                X[a, g][:, u] = xn[g][:, lanes[i]]
            stops[a] = np.count_nonzero(stop)
        P, Q, c = NP, NQ, stops & 255
    yp = np.stack([stand(P, a, VI - 1) for a in range(N)]); yq = np.stack([stand(Q, a, VI - 1) for a in range(N)])
    return {"yp": yp.reshape(N, 128, L).astype(np.float32), "yq": yq.reshape(N, 128, L).astype(np.float32),
            "yx": np.ascontiguousarray(X[..., :D]).reshape(N, 128, D).astype(np.float32).astype(BF)}

@@ -1,0 +1,567 @@
+import numpy as np
+from concourse.bass import DstId, RemoteDMATransfer, IndirectOffsetOnAxis
+from concourse.mybir import dt, AluOpType, AxisListType, ActivationFunctionType
+
+A = AluOpType
+F = ActivationFunctionType
+NR, VI, H, L, D = 8, 4, 64, 128, 1760
+STRIDE = (4, 1)
+XW = 16 + D + 128
+SB = {
+    "X": (XW, "bfloat16"), "R": (16 + D, "int32"), "dr0": (L, "int32"), "wy0": (L, "int32"), "lmI": (1, "int32"),
+    "kI": (1, "int32"), "aI": (1, "int32"), "gI": (1, "int32"), "kc": (1, "float32"), "ac": (1, "float32"), "gc": (1, "float32"),
+    "cid": (128, "float32"), "mro": (128, "float32"), "gro": (128, "float32"), "g8": (8, "float32"), "j16": (16, "float32"),
+    "I32": (128, "float32"), "I16": (128, "float16"), "Ib": (128, "bfloat16"), "I16b": (128, "bfloat16"), "Im16": (128, "float16"),
+    "bo": (128, "bfloat16"), "bo32": (128, "float32"), "bo256": (128, "bfloat16"),
+    "bo8": (8, "bfloat16"), "bo8f": (8, "float32"), "bo8h": (8, "float16"), "wm16": (8, "bfloat16"), "w32": (8, "bfloat16"), "bo8a": (8, "bfloat16"), "bo8b": (8, "bfloat16"),
+    "on": (128, "bfloat16"), "on32": (128, "float32"), "on16": (128, "float16"), "tie16": (128, "bfloat16"),
+    "m15": (16, "float32"), "m16": (16, "float16"), "eqm": (128, "bfloat16"), "cm": (128, "bfloat16"), "cm2": (128, "float32"), "cm3": (128, "float32"),
+    "d0m": (128, "float32"), "d0s": (128, "float32"), "d0p": (128, "float32"), "d0b": (2048, "bfloat16"),
+    "pw2": (16, "float32"), "one16": (16, "float32"), "pwo": (16, "float32"), "m64": (1, "float32"), "dum": (1, "float32"),
+    "bit": (128, "float32"), "tri": (512, "float16"), "limb": (8, "float32"), "limf": (1, "float32"), "lim8": (8, "float32"),
+    "pof": (128, "float32"), "pofI": (128, "int32"), "pof16": (128, "float16"),
+    "IF": (2048, "bfloat16"), "PA": (2048, "bfloat16"), "PB": (2048, "bfloat16"), "CA": (2048, "bfloat16"), "CB": (2048, "bfloat16"),
+    "LW": (2048, "bfloat16"), "LB": (2048, "bfloat16"), "lf": (128, "float32"), "lu1": (128, "uint16"), "lu2": (128, "uint16"), "lu4": (128, "uint16"), "lu8": (128, "uint16"),
+    "qf0": (128, "float32"), "fil": (128, "float32"), "a0": (128, "float32"), "w0": (128, "float32"),
+    "x": (2048, "bfloat16"), "x2": (2048, "bfloat16"), "xc": (2048, "bfloat16"), "mn": (2048, "bfloat16"), "vf": (2048, "bfloat16"), "bs": (2048, "float16"),
+    "eR": (128, "bfloat16"), "e2": (128, "bfloat16"), "q16": (128, "float16"), "aa": (128, "int32"), "aF": (128, "float32"), "aM": (128, "float32"),
+    "n0": (8, "float32"), "n1": (8, "float32"), "n2": (8, "float32"), "thr": (8, "float32"), "mx": (128, "float32"), "sm": (128, "float32"), "stp": (8, "float32"),
+    "oh": (128, "float32"), "pw": (128, "float32"), "pr": (128, "int32"), "bb": (128, "int32"), "q2P": (128, "float16"), "q2u": (128, "uint16"), "q2h": (128, "float16"),
+    "fR": (128, "bfloat16"), "vv": (128, "float32"), "lo": (128, "float16"), "u1": (128, "float16"), "eP": (128, "float32"), "eQ": (128, "float32"),
+    "mk": (128, "float32"), "zi": (8, "int32"), "r16": (8, "float32"), "ok": (128, "float16"), "pk": (128, "float32"), "sk": (128, "float32"), "AL": (128, "float16"), "lk": (8, "uint16"),
+    "cd": (128, "uint16"), "cd16": (128, "float16"), "oka": (128, "float32"), "t3": (128, "float32"),
+    "ms": (128, "float32"), "oj": (128, "float32"), "pn": (128, "float32"), "sn": (128, "float32"), "AN": (128, "float16"),
+    "pq": (128, "float32"), "on1": (128, "float32"), "xk": (128, "float32"), "ky": (128, "float32"), "tief": (128, "float32"), "sq": (128, "float32"), "dg": (1024, "float16"), "eq": (1024, "bfloat16"), "du": (8, "float32"), "uu": (8, "float32"), "ut": (8, "float32"), "of": (8, "float32"), "AS": (128, "float16"), "ls": (8, "uint16"),
+    "tf": (128, "float32"), "ti": (128, "int32"), "xs": (128, "float32"), "xn": (128, "int32"), "cn": (1, "float32"), "ci": (1, "int32"), "cj": (1, "int32"), "c16": (1, "float32"),
+    "yt": (128, "float32"), "yo": (128, "float32"), "vI": (128, "int32"), "yw": (128, "float32"),
+}
+ALONE = ("X", "R", "dr0", "wy0", "lmI", "yt", "yw")
+ALIAS, SCRATCH, _wide = {}, {}, {}
+for _k, (_w, _d) in SB.items():
+    if _w > 1024 or _k in ALONE:
+        SCRATCH[_k] = ("sbuf", [128, _w], _d)
+    else:
+        ALIAS[_k] = ("p_" + _d, _wide.get(_d, 0))
+        _wide[_d] = _wide.get(_d, 0) + -(-_w // 16) * 16
+for _d, _w in _wide.items():
+    SCRATCH["p_" + _d] = ("sbuf", [128, _w], _d)
+for _t in range(VI):
+    SCRATCH["q%d" % _t] = ("sbuf", [128, L], "uint16")
+    SCRATCH["v%d" % _t] = ("sbuf", [128, L], "int32")
+for _t in range(1, VI):
+    SCRATCH["qo%d" % _t] = ("sbuf", [128, L], "uint16")
+    SCRATCH["vo%d" % _t] = ("sbuf", [128, L], "int32")
+    SCRATCH["rq%d" % _t] = ("sbuf", [128, H], "uint16")
+    SCRATCH["rv%d" % _t] = ("sbuf", [128, H], "int32")
+PS = ("pW", "pT", "pU", "pS", "pQ", "pA", "pL", "pD")
+for _p in PS:
+    SCRATCH[_p] = ("psum", [128, 512], "float32")
+SEMAPHORES = ["ev", "es", "et", "eg", "loc"] + ["ld%d" % _t for _t in range(5)] + ["st%d" % _t for _t in range(3)]
+for _t in range(1, VI):
+    SEMAPHORES += ["%s%d" % (_n, _t) for _n in ("qL", "qH", "vL", "vH", "rq", "rv")]
+
+
+def relay_of(core, dst, topo):
+    c = [k for k in topo.cores_of(core) if k != core and topo.may_write(k, dst)]
+    return ([k for k in c if topo.die(k) == topo.die(core)] + c)[0]
+
+
+def engs(src, dst, n, top=False):
+    return src, dst, n, top
+
+
+def bits(topo, src, dst, n, top):
+    e = topo.engines(src, dst)
+    e = e[len(e) - n:] if top else e[:n]
+    return sum(1 << k for k in e)
+
+
+def rank_program(g, core, T, topo):
+    rank = T.rank_of(core)
+    if rank is None:
+        for r, c in enumerate(T.cores):
+            dst = T.cores[(r + STRIDE[1]) % NR]
+            if relay_of(c, dst, topo) == core:
+                relay(g, core, dst, T, topo)
+        return
+    member(g, core, rank, T, topo)
+
+
+def relay(g, core, dst, T, topo):
+    rid, pid = topo.addr(dst, core)
+    m = bits(topo, core, dst, 8, False)
+    n = 0
+    for t in range(1, VI):
+        for k in ("v", "q"):
+            g.wait_ge(T.sem["r%s%d" % (k, t)], 8)
+            g.remote_dma(T["%s%d" % (k, t)][:, H:L], T["r%s%d" % (k, t)][:, :], T.sem["%sH%d" % (k, t)], T.sem["loc"], pid, rid, m)
+            n += 8
+    g.wait_ge(T.sem["loc"], n)
+
+
+def member(g, core, rank, T, topo):
+    Q = {"v": g.vector, "s": g.scalar, "t": g.tensor, "g": g, "y": g.sync}
+    ES = {"v": "ev", "s": "es", "t": "et", "g": "eg"}
+    cnt = {}
+    known = {q: {} for q in Q}
+    snap = {}
+    recs = {}
+    psum = set(PS)
+
+    def vw(name, lo=0, hi=None, st=1, r0=0, r1=128):
+        if hi is None:
+            hi = SB[name][0] if name in SB else SCRATCH[name][1][1]
+        if name in ALIAS:
+            name, o = ALIAS[name]
+            lo, hi = lo + o, hi + o
+        ap = T[name][r0:r1, lo:hi:st] if st > 1 else T[name][r0:r1, lo:hi]
+        return {"ap": ap, "n": name, "lo": lo, "hi": hi, "st": st, "x": None}
+
+    def ind(w, o):
+        return {"ap": w["ap"].indirect(o["ap"]), "n": w["n"], "lo": w["lo"], "hi": w["hi"], "st": 1, "x": o}
+
+    def clash(a, b):
+        if a["n"] in psum:
+            return True
+        if a["lo"] >= b["hi"] or b["lo"] >= a["hi"]:
+            return False
+        return not (a["st"] > 1 and a["st"] == b["st"] and (a["lo"] - b["lo"]) % a["st"])
+
+    def need(q, tok):
+        s, n = tok
+        if known[q].get(s, 0) >= n:
+            return
+        Q[q].wait_ge(T.sem[s], n)
+        known[q][s] = n
+        for k, m in snap.get(tok, {}).items():
+            if known[q].get(k, 0) < m:
+                known[q][k] = m
+
+    def expand(vs):
+        r = []
+        for a in vs:
+            if isinstance(a, dict):
+                r.append(a)
+                if a["x"]:
+                    r.append(a["x"])
+        return r
+
+    def deps(q, outs, ins):
+        want = []
+        for a, wr in [(a, True) for a in outs] + [(a, False) for a in ins]:
+            for b, bw, tok, bq in recs.get(a["n"], []):
+                if not clash(a, b):
+                    continue
+                if a["n"] in psum:
+                    over = not (a["lo"] >= b["hi"] or b["lo"] >= a["hi"])
+                    if bq == q and (q == "t" or not (over and bw and not wr)):
+                        continue
+                else:
+                    if not wr and not bw:
+                        continue
+                    if bq == q and q != "y" and not bw:
+                        continue
+                want.append(tok)
+        best = {}
+        for s, n in want:
+            best[s] = max(best.get(s, 0), n)
+        for s in sorted(best):
+            need(q, (s, best[s]))
+
+    def note(q, tok, outs, ins):
+        for a, wr in [(a, True) for a in outs] + [(a, False) for a in ins]:
+            l = recs.setdefault(a["n"], [])
+            if wr and a["st"] == 1 and a["n"] not in psum:
+                l[:] = [b for b in l if not (a["lo"] <= b[0]["lo"] and b[0]["hi"] <= a["hi"])]
+            elif a["n"] in psum or not wr:
+                l[:] = [b for b in l if not (b[3] == q and b[1] == wr and b[0]["lo"] == a["lo"] and b[0]["hi"] == a["hi"] and b[0]["st"] == a["st"])]
+            l.append((a, wr, tok, q))
+
+    def op(q, outs, ins, fn, sem=None, inc=1):
+        ins = expand(ins + [a["x"] for a in outs])
+        deps(q, outs, ins)
+        s = sem or ES[q]
+        fn().then_inc(T.sem[s], inc)
+        cnt[s] = cnt.get(s, 0) + inc
+        tok = (s, cnt[s])
+        snap[tok] = dict(known[q])
+        note(q, tok, outs, ins)
+
+    def P(a):
+        return a["ap"] if isinstance(a, dict) else a
+
+    def outview(o):
+        return [o]
+
+    def copy(o, i, q="v"):
+        op("v", [o], [i], lambda: g.vector.tensor_copy(P(o), P(i)))
+
+    def tt(o, a, b, f):
+        op("v", [o], [a, b], lambda: g.vector.tensor_tensor(P(o), P(a), P(b), f))
+
+    def ts(o, a, s1, f1, s2=None, f2=None):
+        if s2 is None:
+            op("v", [o], [a, s1], lambda: g.vector.tensor_scalar(P(o), P(a), P(s1), None, f1))
+        else:
+            op("v", [o], [a, s1, s2], lambda: g.vector.tensor_scalar(P(o), P(a), P(s1), P(s2), f1, f2))
+
+    def scan(o, d0, d1, f0, f1, init=0.0):
+        op("v", [o], [d0, d1], lambda: g.vector.tensor_tensor_scan(P(o), P(d0), P(d1), init, f0, f1))
+
+    def fill(o, c):
+        op("v", [o], [], lambda: g.vector.memset(P(o), c))
+
+    def act(o, i, scale=1.0, bias=0.0):
+        op("s", [o], [i, scale], lambda: g.scalar.activation(P(o), P(i), F.Identity, bias=bias, scale=P(scale)))
+
+    def mm(o, a, b, start=True, stop=True):
+        op("t", [o], [a, b], lambda: g.tensor.matmul(P(o), P(a), P(b), start, stop))
+
+    def load(o, src, sem, q="y"):
+        op(q, [o], [], lambda: Q[q].dma_start(P(o), src), sem, 16)
+
+    def store(dst, i, sem, q="y"):
+        op(q, [], [i], lambda: Q[q].dma_start(dst, P(i)), sem, 16)
+
+    load(vw("wy0"), T.why[:, :], "ld0")
+    load(vw("dr0"), T.drugs[:, :], "ld1", "s")
+    load(vw("X", 16, 16 + D), T.eff[:, :], "ld2")
+    load(vw("lmI"), T.lim[:, :], "ld3", "s")
+    load(vw("R", 16, 16 + D), T.rem[:, :], "ld4")
+
+    def iota(o, pat, base, cm, fl=True):
+        op("g", [o], [], lambda: g.iota(P(o), pat, base, cm, allow_small_or_imprecise_dtypes=True) if fl else g.iota(P(o), pat, base, cm))
+    iota(vw("kI"), [[1, 1]], 0, 1, False)
+    iota(vw("mro"), [[0, 8], [1, 16]], 0, 0)
+    iota(vw("pofI"), [[0, 2], [16, 64]], 0, 0, False)
+    iota(vw("g8"), [[1, 8]], 0, 0)
+    iota(vw("cid"), [[1, 128]], 0, 0)
+    iota(vw("gro"), [[1, 8], [0, 16]], 0, 0)
+    ts(vw("aI"), vw("kI"), 15, A.bitwise_and)
+    ts(vw("gI"), vw("kI"), 4, A.arith_shift_right)
+    copy(vw("kc"), vw("kI"))
+    copy(vw("ac"), vw("aI"))
+    copy(vw("gc"), vw("gI"))
+    ts(vw("eqm"), vw("mro"), vw("ac"), A.is_equal)
+    for h in range(0, 2048, 128):
+        if h == 0:
+            copy(vw("IF", 0, 128), vw("eqm"))
+        elif h & (h - 1) == 0:
+            copy(vw("IF", h, 2 * h), vw("IF", 0, h))
+    tt(vw("lf"), vw("wy0"), vw("pofI"), A.add)
+    copy(vw("lu1"), vw("lf"))
+    HV = ((0, 64), (64, 128))
+
+    def pgath(q, dst, src, lst, h):
+        o, w, f = vw(dst, 1024 * h, 1024 * h + 1024), vw(src, 1024 * h, 1024 * h + 1024), vw(lst, *HV[h])
+        if q == "s":
+            act(o, ind(w, f))
+        else:
+            copy(o, ind(w, f))
+
+    def cgath(dst, src, lst, h):
+        o, w, f = vw(dst, 1024 * h, 1024 * h + 1024), vw(src, 1024 * h, 1024 * h + 1024), vw(lst, *HV[h])
+        d = vw("xc", 1024 * h, 1024 * h + 1024)
+        if src == "IF":
+            tt(o, vw("PA", 1024 * h, 1024 * h + 1024), w, A.max)
+        else:
+            act(d, w) if lst == "lu8" else copy(d, w)
+            tt(o, ind(w, f), d, A.max)
+
+    def xgath(q, dst, lst, c0, c1, conv=False, lo=0):
+        o, w, f = vw(dst, 16 * c0, 16 * c1), vw("X", lo, 16 + D), vw(lst, c0, c1)
+        if q == "s":
+            act(o, ind(w, f), 16.0, -2048.0) if conv else act(o, ind(w, f))
+        elif conv:
+            ts(o, ind(w, f), 16.0, A.mult, -2048.0, A.add)
+        else:
+            copy(o, ind(w, f))
+    pgath("s", "PA", "IF", "lu1", 0)
+    pgath("v", "PA", "IF", "lu1", 1)
+    pgath("s", "PB", "PA", "lu1", 0)
+    ts(vw("bo8"), vw("g8"), vw("gc"), A.is_equal)
+    ts(vw("bo8a"), vw("bo8"), vw("ac"), A.mult)
+    fill(vw("LW"), 0.0)
+    for m in range(16):
+        (act if m % 2 else copy)(vw("LW", 128 * m + m, 128 * m + 128, 16), vw("bo8a"))
+    ts(vw("I32"), vw("cid"), vw("kc"), A.is_equal)
+    copy(vw("I16"), vw("I32"))
+    copy(vw("pof16"), vw("pofI"))
+    pgath("v", "PB", "PA", "lu1", 1)
+
+    def conv(src, lst, h):
+        o = vw("pU" if h == 0 else "pS", 0, 64)
+        mm(o, vw("I16"), vw("pof16", *HV[h]), True, False)
+        for m in range(16):
+            mm(o, vw("LW", 128 * m, 128 * m + 128), vw(src, 1024 * h + m, 1024 * h + 1024, 16), False, m == 15)
+        copy(vw(lst, *HV[h]), o)
+    cgath("CA", "IF", "lu1", 0)
+    conv("PB", "lu2", 0)
+    conv("PB", "lu2", 1)
+    pgath("s", "mn", "PB", "lu2", 0)
+    pgath("s", "mn", "PB", "lu2", 1)
+    ts(vw("fil"), vw("dr0"), D, A.is_lt)
+    ts(vw("qf0"), vw("dr0"), 16, A.add)
+    tt(vw("qf0"), vw("qf0"), vw("fil"), A.mult)
+    copy(vw("q0"), vw("qf0"))
+    fill(vw("X", 0, 16), -1.0)
+    fill(vw("X", 16 + D, XW), 0.0)
+    fill(vw("R", 0, 16), 0)
+    cgath("CA", "IF", "lu1", 1)
+    cgath("CB", "CA", "lu2", 0)
+    conv("mn", "lu4", 0)
+    cgath("CB", "CA", "lu2", 1)
+    conv("mn", "lu4", 1)
+    pgath("s", "PB", "mn", "lu4", 0)
+    pgath("s", "PB", "mn", "lu4", 1)
+    iota(vw("j16"), [[1, 16]], 0, 0)
+    ts(vw("pw2"), vw("j16"), vw("ac"), A.is_lt, 1.0, A.add)
+    fill(vw("one16"), 1.0)
+    scan(vw("pwo"), vw("pw2"), vw("one16"), A.mult, A.mult, 1.0)
+    pcol = vw("pwo", 15, 16)
+    ts(vw("bo8b"), vw("bo8"), pcol, A.mult)
+    fill(vw("LB"), 0.0)
+    for m in range(16):
+        act(vw("LB", 128 * m + m, 128 * m + 128, 16), vw("bo8b"))
+    xgath("s", "x", "q0", 0, 64)
+    xgath("s", "x", "q0", 64, 128)
+    cgath("CA", "CB", "lu4", 0)
+    conv("PB", "lu8", 0)
+    cgath("CA", "CB", "lu4", 1)
+    conv("PB", "lu8", 1)
+    fill(vw("on"), 1.0)
+    fill(vw("on32"), 1.0)
+    fill(vw("on16"), 1.0)
+    copy(vw("Ib"), vw("I32"))
+    ts(vw("I16b"), vw("I32"), 16.0, A.mult)
+    ts(vw("Im16"), vw("I32"), -16.0, A.mult)
+    ts(vw("bo32"), vw("gro"), vw("gc"), A.is_equal)
+    copy(vw("bo"), vw("bo32"))
+    ts(vw("bo256"), vw("bo32"), 256.0, A.mult)
+    copy(vw("bo8h"), vw("bo8"))
+    ts(vw("wm16"), vw("bo8"), -16.0, A.mult)
+    ts(vw("w32"), vw("bo8"), 32.0, A.mult)
+    ts(vw("m15"), vw("mro", 0, 16), -1.0, A.mult, 15.0, A.add)
+    ts(vw("tief"), vw("mro"), -1.0, A.mult, 15.0, A.add)
+    ts(vw("tie16"), vw("mro"), -16.0, A.mult, 240.0, A.add)
+    copy(vw("m16"), vw("eqm", 0, 16))
+    fill(vw("d0m"), 0.0)
+    fill(vw("d0m", 0, 128, 16), -16777216.0)
+    fill(vw("d0s"), 1.0)
+    fill(vw("d0s", 0, 128, 16), 0.0)
+    ts(vw("d0p"), vw("d0s"), 2.0, A.mult)
+    fill(vw("d0b"), 1.0)
+    fill(vw("d0b", 0, 2048, 16), -8192.0)
+    copy(vw("limf"), vw("lmI"))
+    ts(vw("lim8"), vw("I32", 0, 128, 16), vw("limf"), A.mult)
+    cgath("CB", "CA", "lu8", 0)
+    cgath("CB", "CA", "lu8", 1)
+    mm(vw("pT", 256, 264), vw("on32"), vw("lim8"))
+    copy(vw("limb"), vw("pT", 256, 264))
+    for h in (0, 1):
+        for m in range(16):
+            mm(vw("pA", 384 + 64 * h, 448 + 64 * h), vw("LB", 128 * m, 128 * m + 128), vw("CB", 1024 * h + m, 1024 * h + 1024, 16), m == 0, m == 15)
+    tt(vw("aF"), vw("pA", 384, 512), vw("fil"), A.mult)
+    ts(vw("w0"), vw("wy0"), 65536.0, A.mult)
+    tt(vw("v0"), vw("aF"), vw("w0"), A.add)
+
+    def late_constants():
+        ts(vw("cm"), vw("mro"), vw("ac"), A.is_equal)
+        ts(vw("cm2"), vw("mro"), vw("ac"), A.is_gt, 64.0, A.mult)
+        ts(vw("cm3"), vw("cm"), -32.0, A.mult, 1.0, A.add)
+        tt(vw("cm2"), vw("cm2"), vw("cm3"), A.add)
+        tt(vw("cm"), vw("cm2"), vw("bo32"), A.mult)
+        ts(vw("m64"), vw("ac"), 65536.0, A.mult)
+        ts(vw("bit"), vw("on32"), pcol, A.mult)
+        ts(vw("dum"), vw("kc"), float(16 + D), A.add)
+        for b in range(4):
+            ts(vw("tri", 128 * b, 128 * b + 128), vw("cid"), vw("kc"), A.is_le, 4096.0, A.mult)
+
+    def dedupe():
+        for b in (0, 1):
+            for w in range(4 * b, 4 * b + 4):
+                ts(vw("dg", 128 * w, 128 * w + 128), vw("I16"), vw("sq", 16 * w + 15, 16 * w + 16), A.mult)
+            mm(vw("pD"), vw("I16"), vw("tri"), True, False)
+            mm(vw("pD"), vw("on16"), vw("dg", 512 * b, 512 * b + 512), False, True)
+            for w in range(4 * b, 4 * b + 4):
+                ts(vw("eq", 128 * w, 128 * w + 128), vw("pD", 128 * (w - 4 * b), 128 * (w - 4 * b) + 128), vw("sq", 16 * w + 15, 16 * w + 16), A.is_equal)
+        for w in range(8):
+            mm(vw("pL", 272 + w, 273 + w), vw("eq", 128 * w, 128 * w + 128), vw("on", 0, 1))
+        ts(vw("du"), vw("pL", 272, 280), 0.5, A.is_lt)
+        tt(vw("uu"), vw("du"), vw("sq", 15, 128, 16), A.mult)
+        ts(vw("ut"), vw("uu"), 0.0, A.is_equal, vw("dum"), A.mult)
+        tt(vw("of"), vw("uu"), vw("ut"), A.add)
+        for w in range(8):
+            ts(vw("AS", 16 * w, 16 * w + 16), vw("m16"), vw("of", w, w + 1), A.mult)
+        mm(vw("pL", 264, 272), vw("AS"), vw("bo8h"))
+        copy(vw("ls"), vw("pL", 264, 272))
+        tt(vw("xs"), ind(vw("X"), vw("ls")), vw("ti"), A.add)
+        ts(vw("xn"), vw("xs"), 0.5, A.mult, -0.25, A.add)
+
+    def scatter():
+        copy(ind(vw("X"), vw("ls")), vw("xn"))
+
+    def stops():
+        mm(vw("pT", 128, 136), vw("on32"), vw("stp"))
+        o, i = vw("cn"), vw("pT", 128, 136)
+        op("v", [o], [i], lambda: g.vector.tensor_reduce(P(o), P(i), AxisListType.X, A.add))
+        copy(vw("ci"), vw("cn"))
+        ts(vw("cj"), vw("ci"), 255, A.bitwise_and)
+        copy(vw("c16"), vw("cj"))
+
+    for t in range(VI):
+        q, v = "q%d" % t, "v%d" % t
+        if t:
+            for k, h in (("q", 0), ("v", 0), ("q", 1), ("v", 1)):
+                s = "%s%s%d" % (k, "LH"[h], t)
+                cnt[s] = 8
+                snap[(s, 8)] = {}
+                recs.setdefault("%s%d" % (k, t), []).append((vw("%s%d" % (k, t), *HV[h]), True, (s, 8), "remote"))
+            xgath("v", "x", q, 0, 32)
+            xgath("s", "x", q, 32, 64)
+            xgath("v", "x", q, 64, 96)
+            xgath("s", "x", q, 96, 128)
+        ts(vw("eR"), vw(q), 0, A.is_equal)
+        ts(vw("q16"), vw(q), 0.0, A.add)
+        if t:
+            ts(vw("aa"), vw(v), 65535, A.bitwise_and)
+            copy(vw("aF"), vw("aa"))
+        for c in range(4):
+            for m in range(16):
+                mm(vw("pW", m, 128, 16, 32 * c, 32 * c + 32), vw("x", 512 * c + m, 512 * c + 512, 16), vw("bo8"))
+        mm(vw("pT", 256, 264), vw("eR"), vw("bo8"))
+        ts(vw("n0"), vw("pT", 256, 264), 0.0, A.is_equal, -4194304.0, A.mult)
+        ts(vw("n1"), vw("pT", 256, 264), -16.0, A.mult, vw("c16") if t else 0.0, A.add)
+        tt(vw("n2"), vw("n1"), vw("limb"), A.add)
+        tt(vw("thr"), vw("n2"), vw("n0"), A.add)
+        mm(vw("pA", 0, 128), vw("aF"), vw("I32"))
+        mm(vw("pQ", 0, 128), vw("q16"), vw("I16"))
+        key = vw("pW", 0, 128)
+        scan(vw("sm"), vw("d0s"), key, A.mult, A.add)
+        scan(vw("mx"), vw("d0m"), key, A.add, A.max)
+        tt(vw("stp"), vw("sm", 15, 128, 16), vw("thr"), A.is_ge)
+        for w in range(8):
+            ts(vw("oh", 16 * w, 16 * w + 16), vw("mx", 16 * w, 16 * w + 16), vw("mx", 16 * w + 15, 16 * w + 16), A.is_equal, vw("stp", w, w + 1), A.mult)
+        scan(vw("pw"), vw("d0p"), vw("oh"), A.mult, A.max)
+        for w in range(8):
+            ts(vw("pr", 16 * w, 16 * w + 16), vw("pA", 16 * w, 16 * w + 16), vw("pw", 16 * w + 15, 16 * w + 16), A.mult)
+        ts(vw("bb"), vw("pr"), 32768, A.bitwise_and)
+        tt(vw("q2P"), vw("pQ", 0, 128), vw("bb"), A.subtract)
+        mm(vw("pL", 384, 512), vw("q2P"), vw("I16"))
+        copy(vw("q2u"), vw("pL", 384, 512))
+        xgath("s", "x2", "q2u", 64, 128, True)
+        xgath("v", "x2", "q2u", 0, 64, True)
+        if t == 0:
+            late_constants()
+        ts(vw("e2"), vw("q2u"), 0, A.is_equal)
+        for m in range(16):
+            mm(vw("pT", 0, 128), vw("Ib"), vw("x", m, 2048, 16), m == 0, False)
+        mm(vw("pT", 0, 128), vw("bo"), vw("eR"), False, True)
+        mm(vw("pL", 0, 128), vw("e2"), vw("cm"))
+        mm(vw("pL", 128, 256), vw("cm"), vw("e2"))
+        scan(vw("bs", 0, 1024), vw("d0b", 0, 1024), vw("x2", 0, 1024), A.add, A.max)
+        scan(vw("bs", 1024, 2048), vw("d0b", 1024, 2048), vw("x2", 1024, 2048), A.add, A.max)
+        bl = vw("bs", 15, 2048, 16)
+        ts(vw("lo"), bl, 0.0625, A.mult, 1280 - 0.46875, A.add)
+        ku = vw("pU", 0, 128)
+        mm(ku, vw("on", 0, 128, 1, 0, 1), vw("tie16", 0, 128, 1, 0, 1), True, False)
+        mm(ku, vw("e2"), vw("bo256"), False, False)
+        for m in range(16):
+            mm(ku, vw("x2", m, 2048, 16), vw("I16b"), False, False)
+        mm(ku, bl, vw("I16"), False, False)
+        mm(ku, vw("lo"), vw("Im16"), False, True)
+        ts(vw("eP"), vw("pL", 0, 128), -16.5, A.is_lt)
+        ts(vw("eQ"), vw("pL", 128, 256), -16.5, A.is_lt)
+        ts(vw("q2h"), vw("q2u"), 0.0, A.add)
+        ts(vw("fR"), vw("q2u"), 0, A.is_gt)
+        tt(vw("vv"), vw(v), vw("fR"), A.mult)
+        ts(vw("aM"), vw("aF"), vw("m64"), A.add)
+        ts(vw("ti"), vw("pT", 0, 128), 0.0625, A.mult, -0.46875, A.add)
+        ts(vw("on1"), vw("pw"), 1.0, A.is_equal)
+        tt(vw("pq"), vw("on1"), vw("pQ", 0, 128), A.mult)
+        scan(vw("sq"), vw("d0s"), vw("pq"), A.mult, A.add)
+        ts(vw("u1"), ku, 1.0 / 4096, A.mult, 1156.5 + 1.0 / 8192, A.add)
+        mm(vw("pS", 128, 256), vw("u1"), vw("I16"))
+        for j in range(16):
+            act(vw("vf", j, 2048, 16), vw("pS", 128, 256), -1.0, 1279.0)
+        scan(vw("mk"), vw("d0m"), ku, A.add, A.max)
+        kk = vw("mk", 15, 128, 16)
+        ts(vw("zi"), kk, 0.0625, A.mult, -0.46875, A.add)
+        ts(vw("r16"), vw("zi"), 16.0, A.mult)
+        for w in range(8):
+            ts(vw("ok", 16 * w, 16 * w + 16), vw("m15"), vw("r16", w, w + 1), A.add, vw("mk", 16 * w + 15, 16 * w + 16), A.is_equal)
+        tt(vw("pk"), vw("ok"), vw("pQ", 0, 128), A.mult)
+        scan(vw("sk"), vw("d0s"), vw("pk"), A.mult, A.add)
+        for w in range(8):
+            ts(vw("AL", 16 * w, 16 * w + 16), vw("m16"), vw("sk", 16 * w + 15, 16 * w + 16), A.mult)
+        mm(vw("pL", 256, 264), vw("AL"), vw("bo8h"))
+        copy(vw("lk"), vw("pL", 256, 264))
+        copy(vw("cd"), ind(vw("R"), vw("lk")))
+        xgath("s", "xc", "cd", 0, 128, False, 16)
+        mm(vw("pA", 256, 384), vw("ok"), vw("I16"))
+        if t == VI - 1:
+            dedupe()
+        for c in range(4):
+            tt(vw("mn", 512 * c, 512 * c + 512), ind(vw("X", 16, 16 + D), vw("cd", 32 * c, 32 * c + 32)), vw("vf", 512 * c, 512 * c + 512), A.min)
+            if c == 0:
+                tt(vw("oka"), vw("pA", 256, 384), vw("aM"), A.mult)
+                ts(vw("cd16"), vw("cd"), 16.0, A.add)
+        mm(vw("pA", 128, 256), vw("bo32"), vw("oka"), True, False)
+        mm(vw("pA", 128, 256), vw("I32"), vw("bit"), False, True)
+        mm(vw("pQ", 128, 256), vw("cd16"), vw("I16"))
+        for j in range(16):
+            mm(vw("pW", 256 + j, 384, 16), vw("xc", j, 2048, 16), vw("wm16"))
+        tt(vw("xk"), vw("pW", 256, 384), vw("tief"), A.add)
+        for c in range(4):
+            for j in range(16):
+                mm(vw("pS", j, 128, 16, 32 * c, 32 * c + 32), vw("mn", 512 * c + j, 512 * c + 512, 16), vw("w32"))
+        tt(vw("t3"), vw("pA", 128, 256), vw("eQ"), A.mult)
+        vo = "vo%d" % (t + 1) if t < VI - 1 else "vI"
+        tt(vw(vo), vw("vv"), vw("t3"), A.add)
+
+        def send(k):
+            src = "%so%d" % (k, t + 1)
+            lowd = T.cores[(rank + STRIDE[0]) % NR]
+            hid = relay_of(core, T.cores[(rank + STRIDE[1]) % NR], topo)
+            r1, p1 = topo.addr(lowd, core)
+            r2, p2 = topo.addr(hid, core)
+            tr = [RemoteDMATransfer(dst_ids=[DstId(rid=r1, pnc=p1)], dma_engine_mask=bits(topo, core, lowd, 8, False), remote_sem=T.sem["%sL%d" % (k, t + 1)],
+                                    src=T[src][:, 0:H], dst=T["%s%d" % (k, t + 1)][:, 0:H]),
+                  RemoteDMATransfer(dst_ids=[DstId(rid=r2, pnc=p2)], dma_engine_mask=bits(topo, core, hid, 8, True), remote_sem=T.sem["r%s%d" % (k, t + 1)],
+                                    src=T[src][:, H:L], dst=T["r%s%d" % (k, t + 1)][:, :])]
+            deps("g", [], [vw(src)])
+            g.remote_dma_fused(tr, local_sem=T.sem["loc"])
+            cnt["loc"] = cnt.get("loc", 0) + 16
+        if t < VI - 1:
+            send("v")
+        if t == VI - 1:
+            scatter()
+            store(T.yx[:, :], vw("X", 16, 16 + D), "st0")
+            ts(vw("bb"), vw("vI"), 16, A.arith_shift_right)
+            copy(vw("yw"), vw("bb"))
+            store(T.yq[:, :], vw("yw"), "st1")
+        tt(vw("ky"), vw("pS", 0, 128), vw("xk"), A.add)
+        scan(vw("ms"), vw("d0m"), vw("ky"), A.add, A.max)
+        for w in range(8):
+            ts(vw("oj", 16 * w, 16 * w + 16), vw("ky", 16 * w, 16 * w + 16), vw("ms", 16 * w + 15, 16 * w + 16), A.is_equal)
+        tt(vw("pn"), vw("oj"), vw("pQ", 128, 256), A.mult)
+        scan(vw("sn"), vw("d0s"), vw("pn"), A.mult, A.add)
+        for w in range(8):
+            ts(vw("AN", 16 * w, 16 * w + 16), vw("eP", 16 * w, 16 * w + 16), vw("sn", 16 * w + 15, 16 * w + 16), A.mult)
+        nq = vw("pL", 384, 512)
+        mm(nq, vw("I16"), vw("q2h"), True, False)
+        mm(nq, vw("AN"), vw("I16"), False, True)
+        if t < VI - 1:
+            copy(vw("qo%d" % (t + 1)), nq)
+            send("q")
+            stops()
+            dedupe()
+            scatter()
+        else:
+            ts(vw("yt"), nq, 0.0, A.is_equal, float(16 + D), A.mult)
+            tt(vw("yo"), vw("yt"), nq, A.add)
+            ts(vw("yt"), vw("yo"), -16.0, A.add)
+            store(T.yp[:, :], vw("yt"), "st2")
+    for s in SEMAPHORES:
+        if cnt.get(s):
+            g.wait_ge(T.sem[s], cnt[s])

@@ -7,35 +7,35 @@ F = ActivationFunctionType
 NR, VI, H, L, D = 8, 4, 64, 128, 1760
 STRIDE = (4, 1)
 XW = 16 + D + 128
+f32, b16, h16, i32, u16 = "float32", "bfloat16", "float16", "int32", "uint16"
 SB = {
-    "X": (XW, "bfloat16"), "R": (16 + D, "int32"), "dr0": (L, "int32"), "wy0": (L, "int32"), "lmI": (1, "int32"),
-    "kI": (1, "int32"), "aI": (1, "int32"), "gI": (1, "int32"), "kc": (1, "float32"), "ac": (1, "float32"), "gc": (1, "float32"),
-    "cid": (128, "float32"), "mro": (128, "float32"), "gro": (128, "float32"), "g8": (8, "float32"), "j16": (16, "float32"),
-    "I32": (128, "float32"), "I16": (128, "float16"), "Ib": (128, "bfloat16"), "I16b": (128, "bfloat16"), "Im16": (128, "float16"),
-    "bo": (128, "bfloat16"), "bo32": (128, "float32"), "bo256": (128, "bfloat16"),
-    "bo8": (8, "bfloat16"), "bo8f": (8, "float32"), "bo8h": (8, "float16"), "wm16": (8, "bfloat16"), "w32": (8, "bfloat16"), "bo8a": (8, "bfloat16"), "bo8b": (8, "bfloat16"),
-    "on": (128, "bfloat16"), "on32": (128, "float32"), "on16": (128, "float16"), "tie16": (128, "bfloat16"),
-    "m15": (16, "float32"), "m16": (16, "float16"), "eqm": (128, "bfloat16"), "cm": (128, "bfloat16"), "cm2": (128, "float32"), "cm3": (128, "float32"),
-    "d0m": (128, "float32"), "d0s": (128, "float32"), "d0p": (128, "float32"), "d0b": (2048, "bfloat16"),
-    "pw2": (16, "float32"), "one16": (16, "float32"), "pwo": (16, "float32"), "m64": (1, "float32"), "dum": (1, "float32"),
-    "bit": (128, "float32"), "tri": (512, "float16"), "limb": (8, "float32"), "limf": (1, "float32"), "lim8": (8, "float32"),
-    "pof": (128, "float32"), "pofI": (128, "int32"), "pof16": (128, "float16"),
-    "IF": (2048, "bfloat16"), "PA": (2048, "bfloat16"), "PB": (2048, "bfloat16"), "CA": (2048, "bfloat16"), "CB": (2048, "bfloat16"),
-    "LW": (2048, "bfloat16"), "LB": (2048, "bfloat16"), "lf": (128, "float32"), "lu1": (128, "uint16"), "lu2": (128, "uint16"), "lu4": (128, "uint16"), "lu8": (128, "uint16"),
-    "qf0": (128, "float32"), "fil": (128, "float32"), "a0": (128, "float32"), "w0": (128, "float32"),
-    "x": (2048, "bfloat16"), "x2": (2048, "bfloat16"), "xc": (2048, "bfloat16"), "mn": (2048, "bfloat16"), "vf": (2048, "bfloat16"), "bs": (2048, "float16"),
-    "eR": (128, "bfloat16"), "e2": (128, "bfloat16"), "q16": (128, "float16"), "aa": (128, "int32"), "aF": (128, "float32"), "aM": (128, "float32"),
-    "n0": (8, "float32"), "n1": (8, "float32"), "n2": (8, "float32"), "thr": (8, "float32"), "mx": (128, "float32"), "sm": (128, "float32"), "stp": (8, "float32"),
-    "oh": (128, "float32"), "pw": (128, "float32"), "pr": (128, "int32"), "bb": (128, "int32"), "q2P": (128, "float16"), "q2u": (128, "uint16"), "q2h": (128, "float16"),
-    "fR": (128, "bfloat16"), "vv": (128, "float32"), "lo": (128, "float16"), "u1": (128, "float16"), "eP": (128, "float32"), "eQ": (128, "float32"),
-    "mk": (128, "float32"), "zi": (8, "int32"), "r16": (8, "float32"), "ok": (128, "float16"), "pk": (128, "float32"), "sk": (128, "float32"), "AL": (128, "float16"), "lk": (8, "uint16"),
-    "cd": (128, "uint16"), "cd16": (128, "float16"), "oka": (128, "float32"), "t3": (128, "float32"),
-    "ms": (128, "float32"), "oj": (128, "float32"), "pn": (128, "float32"), "sn": (128, "float32"), "AN": (128, "float16"),
-    "pq": (128, "float32"), "on1": (128, "float32"), "xk": (128, "float32"), "ky": (128, "float32"), "tief": (128, "float32"), "sq": (128, "float32"), "dg": (1024, "float16"), "eq": (1024, "bfloat16"), "du": (8, "float32"), "uu": (8, "float32"), "ut": (8, "float32"), "of": (8, "float32"), "AS": (128, "float16"), "ls": (8, "uint16"),
-    "tf": (128, "float32"), "ti": (128, "int32"), "xs": (128, "float32"), "xn": (128, "int32"), "cn": (1, "float32"), "ci": (1, "int32"), "cj": (1, "int32"), "c16": (1, "float32"),
-    "yt": (128, "float32"), "yo": (128, "float32"), "vI": (128, "int32"), "yw": (128, "float32"),
+    "X": (XW, b16), "R": (16 + D, i32), "dr0": (L, i32), "wy0": (L, i32), "lmI": (1, i32),
+    "kI": (1, i32), "aI": (1, i32), "gI": (1, i32), "kc": (1, f32), "ac": (1, f32), "gc": (1, f32),
+    "cid": (128, f32), "mro": (128, f32), "g8": (8, f32), "j16": (16, f32),
+    "I32": (128, f32), "I16": (128, h16), "Ib": (128, b16), "I16b": (128, b16), "Im16": (128, h16),
+    "bo": (128, b16), "bo32": (128, f32), "bo256": (128, b16),
+    "bo8": (8, b16), "bo8h": (8, h16), "wm16": (8, b16), "w32": (8, b16), "bo8a": (8, b16), "bo8b": (8, b16),
+    "on": (128, b16), "on32": (128, f32), "on16": (128, h16), "tie16": (128, b16), "tief": (128, f32),
+    "m15": (16, f32), "m16": (16, h16), "cm": (128, b16), "d0m": (128, f32), "d0s": (128, f32), "d0p": (128, f32), "d0b": (2048, b16),
+    "pw2": (16, f32), "one16": (16, f32), "pwo": (16, f32), "m64": (1, f32), "dum": (1, f32),
+    "bit": (128, f32), "tri": (512, b16), "limb": (8, f32), "limf": (1, f32), "lim8": (8, f32),
+    "pofI": (128, i32), "pof16": (128, h16),
+    "IF": (1024, b16), "IG": (1024, b16), "PA": (2048, b16), "PB": (2048, b16), "CA": (2048, b16), "CB": (2048, b16),
+    "LW": (2048, b16), "lf": (128, f32), "lu1": (128, u16), "lu2": (128, u16), "lu4": (128, u16), "lu8": (128, u16),
+    "qf0": (128, f32), "fil": (128, f32), "aP0": (128, f32), "w0": (128, f32),
+    "x": (2048, b16), "x2": (2048, b16), "xc": (2048, b16), "mn": (2048, b16), "vf": (2048, b16), "bs": (2048, h16),
+    "eR": (128, b16), "e2": (128, b16), "q16": (128, h16), "aa": (128, i32), "aF": (128, f32), "aM": (128, f32),
+    "n0": (8, f32), "n1": (8, f32), "n2": (8, f32), "thr": (8, f32), "mx": (128, f32), "sm": (128, f32), "stp": (8, f32),
+    "oh": (128, f32), "pw": (128, f32), "pr": (128, i32), "bb": (128, i32), "q2P": (128, h16), "q2u": (128, u16), "q2h": (128, h16),
+    "fR": (128, b16), "vv": (128, f32), "lo": (128, h16), "u1": (128, h16), "eP": (128, f32), "eQ": (128, f32),
+    "mk": (128, f32), "zi": (8, i32), "r16": (8, f32), "ok": (128, h16), "pk": (128, f32), "sk": (128, f32), "AL": (128, h16), "lk": (8, u16),
+    "cd": (128, u16), "cd16": (128, h16), "oka": (128, f32), "t3": (128, f32), "xk": (128, f32), "ky": (128, f32),
+    "ms": (128, f32), "oj": (128, f32), "pn": (128, f32), "sn": (128, f32), "AN": (128, h16),
+    "on1": (128, f32), "pq": (128, f32), "sq": (128, f32), "dg": (1024, h16), "eq": (1024, b16), "du": (8, f32), "uu": (8, f32), "ut": (8, f32), "of": (8, f32), "AS": (128, h16), "ls": (8, u16),
+    "ti": (128, i32), "xs": (128, f32), "xn": (128, i32), "cn": (1, f32), "ci": (1, i32), "cj": (1, i32), "c16": (1, f32),
+    "yt": (128, f32), "yo": (128, f32), "vI": (128, i32), "yw": (128, f32),
 }
-ALONE = ("X", "R", "dr0", "wy0", "lmI", "yt", "yw")
+ALONE = ("X", "R", "dr0", "wy0", "lmI", "yt", "yw", "IF", "IG")
 ALIAS, SCRATCH, _wide = {}, {}, {}
 for _k, (_w, _d) in SB.items():
     if _w > 1024 or _k in ALONE:
@@ -46,28 +46,25 @@ for _k, (_w, _d) in SB.items():
 for _d, _w in _wide.items():
     SCRATCH["p_" + _d] = ("sbuf", [128, _w], _d)
 for _t in range(VI):
-    SCRATCH["q%d" % _t] = ("sbuf", [128, L], "uint16")
-    SCRATCH["v%d" % _t] = ("sbuf", [128, L], "int32")
+    SCRATCH["q%d" % _t] = ("sbuf", [128, L], u16)
+    SCRATCH["v%d" % _t] = ("sbuf", [128, L], i32)
 for _t in range(1, VI):
-    SCRATCH["qo%d" % _t] = ("sbuf", [128, L], "uint16")
-    SCRATCH["vo%d" % _t] = ("sbuf", [128, L], "int32")
-    SCRATCH["rq%d" % _t] = ("sbuf", [128, H], "uint16")
-    SCRATCH["rv%d" % _t] = ("sbuf", [128, H], "int32")
+    SCRATCH["qo%d" % _t] = ("sbuf", [128, L], u16)
+    SCRATCH["vo%d" % _t] = ("sbuf", [128, L], i32)
+    SCRATCH["rq%d" % _t] = ("sbuf", [128, H], u16)
+    SCRATCH["rv%d" % _t] = ("sbuf", [128, H], i32)
 PS = ("pW", "pT", "pU", "pS", "pQ", "pA", "pL", "pD")
 for _p in PS:
-    SCRATCH[_p] = ("psum", [128, 512], "float32")
+    SCRATCH[_p] = ("psum", [128, 512], f32)
 SEMAPHORES = ["ev", "es", "et", "eg", "loc"] + ["ld%d" % _t for _t in range(5)] + ["st%d" % _t for _t in range(3)]
 for _t in range(1, VI):
     SEMAPHORES += ["%s%d" % (_n, _t) for _n in ("qL", "qH", "vL", "vH", "rq", "rv")]
+HV = ((0, 64), (64, 128))
 
 
 def relay_of(core, dst, topo):
     c = [k for k in topo.cores_of(core) if k != core and topo.may_write(k, dst)]
     return ([k for k in c if topo.die(k) == topo.die(core)] + c)[0]
-
-
-def engs(src, dst, n, top=False):
-    return src, dst, n, top
 
 
 def bits(topo, src, dst, n, top):
@@ -92,7 +89,7 @@ def relay(g, core, dst, T, topo):
     m = bits(topo, core, dst, 8, False)
     n = 0
     for t in range(1, VI):
-        for k in ("v", "q"):
+        for k in ("q", "v"):
             g.wait_ge(T.sem["r%s%d" % (k, t)], 8)
             g.remote_dma(T["%s%d" % (k, t)][:, H:L], T["r%s%d" % (k, t)][:, :], T.sem["%sH%d" % (k, t)], T.sem["loc"], pid, rid, m)
             n += 8
@@ -147,7 +144,7 @@ def member(g, core, rank, T, topo):
         return r
 
     def deps(q, outs, ins):
-        want = []
+        best = {}
         for a, wr in [(a, True) for a in outs] + [(a, False) for a in ins]:
             for b, bw, tok, bq in recs.get(a["n"], []):
                 if not clash(a, b):
@@ -161,10 +158,7 @@ def member(g, core, rank, T, topo):
                         continue
                     if bq == q and q != "y" and not bw:
                         continue
-                want.append(tok)
-        best = {}
-        for s, n in want:
-            best[s] = max(best.get(s, 0), n)
+                best[tok[0]] = max(best.get(tok[0], 0), tok[1])
         for s in sorted(best):
             need(q, (s, best[s]))
 
@@ -190,10 +184,7 @@ def member(g, core, rank, T, topo):
     def P(a):
         return a["ap"] if isinstance(a, dict) else a
 
-    def outview(o):
-        return [o]
-
-    def copy(o, i, q="v"):
+    def copy(o, i):
         op("v", [o], [i], lambda: g.vector.tensor_copy(P(o), P(i)))
 
     def tt(o, a, b, f):
@@ -211,8 +202,8 @@ def member(g, core, rank, T, topo):
     def fill(o, c):
         op("v", [o], [], lambda: g.vector.memset(P(o), c))
 
-    def act(o, i, scale=1.0, bias=0.0):
-        op("s", [o], [i, scale], lambda: g.scalar.activation(P(o), P(i), F.Identity, bias=bias, scale=P(scale)))
+    def act(o, i, scale=1.0, bias=0.0, func=F.Identity):
+        op("s", [o], [i, scale], lambda: g.scalar.activation(P(o), P(i), func, bias=bias, scale=P(scale)))
 
     def mm(o, a, b, start=True, stop=True):
         op("t", [o], [a, b], lambda: g.tensor.matmul(P(o), P(a), P(b), start, stop))
@@ -223,50 +214,62 @@ def member(g, core, rank, T, topo):
     def store(dst, i, sem, q="y"):
         op(q, [], [i], lambda: Q[q].dma_start(dst, P(i)), sem, 16)
 
+    def iota(o, pat, base, cm, fl=True):
+        op("g", [o], [], lambda: g.iota(P(o), pat, base, cm, allow_small_or_imprecise_dtypes=True) if fl else g.iota(P(o), pat, base, cm))
+
+    def gfill(o, n, c, fl=True):
+        iota(o, [[0, n]], c, 0, fl)
+
+    def sel(o, pat, f, c, base, cm):
+        op("g", [o], [o], lambda: g.affine_select(P(o), P(o), pat, f, c, base, cm))
+
+    def half(name, h):
+        return vw(name, 1024 * h, 1024 * h + 1024)
+
     load(vw("wy0"), T.why[:, :], "ld0")
     load(vw("dr0"), T.drugs[:, :], "ld1", "s")
     load(vw("X", 16, 16 + D), T.eff[:, :], "ld2")
     load(vw("lmI"), T.lim[:, :], "ld3", "s")
     load(vw("R", 16, 16 + D), T.rem[:, :], "ld4")
-
-    def iota(o, pat, base, cm, fl=True):
-        op("g", [o], [], lambda: g.iota(P(o), pat, base, cm, allow_small_or_imprecise_dtypes=True) if fl else g.iota(P(o), pat, base, cm))
     iota(vw("kI"), [[1, 1]], 0, 1, False)
     iota(vw("mro"), [[0, 8], [1, 16]], 0, 0)
     iota(vw("pofI"), [[0, 2], [16, 64]], 0, 0, False)
     iota(vw("g8"), [[1, 8]], 0, 0)
     iota(vw("cid"), [[1, 128]], 0, 0)
-    iota(vw("gro"), [[1, 8], [0, 16]], 0, 0)
+    iota(vw("j16"), [[1, 16]], 0, 0)
+    fill(vw("LW"), 0.0)
     ts(vw("aI"), vw("kI"), 15, A.bitwise_and)
-    ts(vw("gI"), vw("kI"), 4, A.arith_shift_right)
-    copy(vw("kc"), vw("kI"))
     copy(vw("ac"), vw("aI"))
+    ts(vw("IF", 0, 128), vw("mro"), vw("ac"), A.is_equal)
+    for h in (128, 256, 512):
+        copy(vw("IF", h, 2 * h), vw("IF", 0, h))
+    act(vw("IG"), vw("IF"))
+    ts(vw("gI"), vw("kI"), 4, A.arith_shift_right)
     copy(vw("gc"), vw("gI"))
-    ts(vw("eqm"), vw("mro"), vw("ac"), A.is_equal)
-    for h in range(0, 2048, 128):
-        if h == 0:
-            copy(vw("IF", 0, 128), vw("eqm"))
-        elif h & (h - 1) == 0:
-            copy(vw("IF", h, 2 * h), vw("IF", 0, h))
+    copy(vw("kc"), vw("kI"))
+    ts(vw("bo8"), vw("g8"), vw("gc"), A.is_equal)
+    ts(vw("bo8a"), vw("bo8"), vw("ac"), A.mult)
     tt(vw("lf"), vw("wy0"), vw("pofI"), A.add)
     copy(vw("lu1"), vw("lf"))
-    HV = ((0, 64), (64, 128))
+
+    def win(name, h):
+        return vw("IF") if name == "IF" else half(name, h)
 
     def pgath(q, dst, src, lst, h):
-        o, w, f = vw(dst, 1024 * h, 1024 * h + 1024), vw(src, 1024 * h, 1024 * h + 1024), vw(lst, *HV[h])
+        o, w, f = half(dst, h), win(src, h), vw(lst, *HV[h])
         if q == "s":
             act(o, ind(w, f))
         else:
             copy(o, ind(w, f))
 
-    def cgath(dst, src, lst, h):
-        o, w, f = vw(dst, 1024 * h, 1024 * h + 1024), vw(src, 1024 * h, 1024 * h + 1024), vw(lst, *HV[h])
-        d = vw("xc", 1024 * h, 1024 * h + 1024)
-        if src == "IF":
-            tt(o, vw("PA", 1024 * h, 1024 * h + 1024), w, A.max)
-        else:
-            act(d, w) if lst == "lu8" else copy(d, w)
-            tt(o, ind(w, f), d, A.max)
+    def cgath(dst, src, lst, h, by=None):
+        o, w, f = half(dst, h), win(src, h), vw(lst, *HV[h])
+        d = vw("IG") if src == "IF" else half("xc", h)
+        if by == "s":
+            act(d, w)
+        elif by == "v":
+            copy(d, w)
+        tt(o, ind(w, f), d, A.max)
 
     def xgath(q, dst, lst, c0, c1, conv=False, lo=0):
         o, w, f = vw(dst, 16 * c0, 16 * c1), vw("X", lo, 16 + D), vw(lst, c0, c1)
@@ -276,117 +279,121 @@ def member(g, core, rank, T, topo):
             ts(o, ind(w, f), 16.0, A.mult, -2048.0, A.add)
         else:
             copy(o, ind(w, f))
-    pgath("s", "PA", "IF", "lu1", 0)
-    pgath("v", "PA", "IF", "lu1", 1)
-    pgath("s", "PB", "PA", "lu1", 0)
-    ts(vw("bo8"), vw("g8"), vw("gc"), A.is_equal)
-    ts(vw("bo8a"), vw("bo8"), vw("ac"), A.mult)
-    fill(vw("LW"), 0.0)
-    for m in range(16):
-        (act if m % 2 else copy)(vw("LW", 128 * m + m, 128 * m + 128, 16), vw("bo8a"))
-    ts(vw("I32"), vw("cid"), vw("kc"), A.is_equal)
-    copy(vw("I16"), vw("I32"))
-    copy(vw("pof16"), vw("pofI"))
-    pgath("v", "PB", "PA", "lu1", 1)
 
-    def conv(src, lst, h):
+    def conv(src, h):
         o = vw("pU" if h == 0 else "pS", 0, 64)
         mm(o, vw("I16"), vw("pof16", *HV[h]), True, False)
         for m in range(16):
             mm(o, vw("LW", 128 * m, 128 * m + 128), vw(src, 1024 * h + m, 1024 * h + 1024, 16), False, m == 15)
-        copy(vw(lst, *HV[h]), o)
+
+    def convd(lst, h):
+        copy(vw(lst, *HV[h]), vw("pU" if h == 0 else "pS", 0, 64))
+    pgath("s", "PA", "IF", "lu1", 0)
+    pgath("v", "PA", "IF", "lu1", 1)
+    for m in range(16):
+        o = vw("LW", 128 * m + m, 128 * m + 128, 16)
+        act(o, vw("bo8a")) if m % 4 else copy(o, vw("bo8a"))
+    pgath("s", "PB", "PA", "lu1", 0)
+    ts(vw("I32"), vw("cid"), vw("kc"), A.is_equal)
+    copy(vw("I16"), vw("I32"))
+    copy(vw("pof16"), vw("pofI"))
+    pgath("v", "PB", "PA", "lu1", 1)
+    conv("PB", 0)
+    conv("PB", 1)
+    gfill(vw("X", 0, 16), 16, -1)
+    gfill(vw("X", 16 + D, XW), 128, 0)
+    gfill(vw("R", 0, 16), 16, 0, False)
+    gfill(vw("d0b"), 2048, 1)
+    sel(vw("d0b"), [[0, 128], [1, 16]], A.not_equal, -8192.0, 0, 0)
+    for n, c, z in (("d0s", 1, 0.0), ("d0m", 0, -16777216.0), ("d0p", 2, 0.0)):
+        gfill(vw(n), 128, c)
+        sel(vw(n), [[0, 8], [1, 16]], A.not_equal, z, 0, 0)
+    gfill(vw("on32"), 128, 1)
+    gfill(vw("on"), 128, 1)
+    gfill(vw("bo32"), 128, 1)
+    gfill(vw("cm"), 128, 65)
+    sel(vw("cm"), [[1, 128]], A.is_gt, 1.0, 0, -1)
+    sel(vw("cm"), [[1, 128]], A.not_equal, -31.0, 0, -1)
+    for n in ("bo32", "cm"):
+        sel(vw(n), [[-16, 8], [0, 16]], A.is_ge, 0.0, 0, 1)
+        sel(vw(n), [[16, 8], [0, 16]], A.is_ge, 0.0, 15, -1)
+    gfill(vw("tri"), 512, 4096)
+    sel(vw("tri"), [[0, 4], [-1, 128]], A.is_ge, 0.0, 0, 1)
     cgath("CA", "IF", "lu1", 0)
-    conv("PB", "lu2", 0)
-    conv("PB", "lu2", 1)
+    convd("lu2", 0)
     pgath("s", "mn", "PB", "lu2", 0)
-    pgath("s", "mn", "PB", "lu2", 1)
+    conv("mn", 0)
+    convd("lu2", 1)
+    cgath("CA", "IF", "lu1", 1)
     ts(vw("fil"), vw("dr0"), D, A.is_lt)
     ts(vw("qf0"), vw("dr0"), 16, A.add)
     tt(vw("qf0"), vw("qf0"), vw("fil"), A.mult)
     copy(vw("q0"), vw("qf0"))
-    fill(vw("X", 0, 16), -1.0)
-    fill(vw("X", 16 + D, XW), 0.0)
-    fill(vw("R", 0, 16), 0)
-    cgath("CA", "IF", "lu1", 1)
-    cgath("CB", "CA", "lu2", 0)
-    conv("mn", "lu4", 0)
-    cgath("CB", "CA", "lu2", 1)
-    conv("mn", "lu4", 1)
+    pgath("s", "mn", "PB", "lu2", 1)
+    conv("mn", 1)
+    cgath("CB", "CA", "lu2", 0, "v")
+    convd("lu4", 0)
+    act(half("xc", 1), half("CA", 1))
     pgath("s", "PB", "mn", "lu4", 0)
+    conv("PB", 0)
+    cgath("CB", "CA", "lu2", 1)
+    convd("lu4", 1)
     pgath("s", "PB", "mn", "lu4", 1)
-    iota(vw("j16"), [[1, 16]], 0, 0)
+    conv("PB", 1)
+    xgath("s", "x", "q0", 0, 64)
     ts(vw("pw2"), vw("j16"), vw("ac"), A.is_lt, 1.0, A.add)
     fill(vw("one16"), 1.0)
     scan(vw("pwo"), vw("pw2"), vw("one16"), A.mult, A.mult, 1.0)
     pcol = vw("pwo", 15, 16)
     ts(vw("bo8b"), vw("bo8"), pcol, A.mult)
-    fill(vw("LB"), 0.0)
-    for m in range(16):
-        act(vw("LB", 128 * m + m, 128 * m + 128, 16), vw("bo8b"))
-    xgath("s", "x", "q0", 0, 64)
+    cgath("CA", "CB", "lu4", 0, "v")
+    convd("lu8", 0)
+    act(half("xc", 0), half("CA", 0))
+    cgath("CA", "CB", "lu4", 1, "v")
+    convd("lu8", 1)
+    act(half("xc", 1), half("CA", 1))
     xgath("s", "x", "q0", 64, 128)
-    cgath("CA", "CB", "lu4", 0)
-    conv("PB", "lu8", 0)
-    cgath("CA", "CB", "lu4", 1)
-    conv("PB", "lu8", 1)
-    fill(vw("on"), 1.0)
-    fill(vw("on32"), 1.0)
-    fill(vw("on16"), 1.0)
-    copy(vw("Ib"), vw("I32"))
-    ts(vw("I16b"), vw("I32"), 16.0, A.mult)
-    ts(vw("Im16"), vw("I32"), -16.0, A.mult)
-    ts(vw("bo32"), vw("gro"), vw("gc"), A.is_equal)
-    copy(vw("bo"), vw("bo32"))
-    ts(vw("bo256"), vw("bo32"), 256.0, A.mult)
-    copy(vw("bo8h"), vw("bo8"))
-    ts(vw("wm16"), vw("bo8"), -16.0, A.mult)
-    ts(vw("w32"), vw("bo8"), 32.0, A.mult)
-    ts(vw("m15"), vw("mro", 0, 16), -1.0, A.mult, 15.0, A.add)
-    ts(vw("tief"), vw("mro"), -1.0, A.mult, 15.0, A.add)
-    ts(vw("tie16"), vw("mro"), -16.0, A.mult, 240.0, A.add)
-    copy(vw("m16"), vw("eqm", 0, 16))
-    fill(vw("d0m"), 0.0)
-    fill(vw("d0m", 0, 128, 16), -16777216.0)
-    fill(vw("d0s"), 1.0)
-    fill(vw("d0s", 0, 128, 16), 0.0)
-    ts(vw("d0p"), vw("d0s"), 2.0, A.mult)
-    fill(vw("d0b"), 1.0)
-    fill(vw("d0b", 0, 2048, 16), -8192.0)
+    act(vw("Ib"), vw("I32"))
+    act(vw("wm16"), vw("bo8"), -16.0)
+    act(vw("w32"), vw("bo8"), 32.0)
+    act(vw("bo"), vw("bo32"))
+    act(vw("I16b"), vw("I32"), 16.0)
+    act(vw("bo256"), vw("bo32"), 256.0)
+    act(vw("tie16"), vw("mro"), -16.0, 240.0)
+    act(vw("tief"), vw("mro"), -1.0, 15.0)
+    act(vw("m15"), vw("mro", 0, 16), -1.0, 15.0)
+    act(vw("bit"), vw("on32"), pcol)
     copy(vw("limf"), vw("lmI"))
     ts(vw("lim8"), vw("I32", 0, 128, 16), vw("limf"), A.mult)
     cgath("CB", "CA", "lu8", 0)
     cgath("CB", "CA", "lu8", 1)
-    mm(vw("pT", 256, 264), vw("on32"), vw("lim8"))
-    copy(vw("limb"), vw("pT", 256, 264))
-    for h in (0, 1):
-        for m in range(16):
-            mm(vw("pA", 384 + 64 * h, 448 + 64 * h), vw("LB", 128 * m, 128 * m + 128), vw("CB", 1024 * h + m, 1024 * h + 1024, 16), m == 0, m == 15)
-    tt(vw("aF"), vw("pA", 384, 512), vw("fil"), A.mult)
-    ts(vw("w0"), vw("wy0"), 65536.0, A.mult)
-    tt(vw("v0"), vw("aF"), vw("w0"), A.add)
 
     def late_constants():
-        ts(vw("cm"), vw("mro"), vw("ac"), A.is_equal)
-        ts(vw("cm2"), vw("mro"), vw("ac"), A.is_gt, 64.0, A.mult)
-        ts(vw("cm3"), vw("cm"), -32.0, A.mult, 1.0, A.add)
-        tt(vw("cm2"), vw("cm2"), vw("cm3"), A.add)
-        tt(vw("cm"), vw("cm2"), vw("bo32"), A.mult)
+        fill(vw("on16"), 1.0)
+        ts(vw("Im16"), vw("I32"), -16.0, A.mult)
+        copy(vw("bo8h"), vw("bo8"))
+        copy(vw("m16"), vw("IF", 0, 16))
         ts(vw("m64"), vw("ac"), 65536.0, A.mult)
-        ts(vw("bit"), vw("on32"), pcol, A.mult)
         ts(vw("dum"), vw("kc"), float(16 + D), A.add)
-        for b in range(4):
-            ts(vw("tri", 128 * b, 128 * b + 128), vw("cid"), vw("kc"), A.is_le, 4096.0, A.mult)
+
+    def stopped():
+        ts(vw("on1"), vw("pw"), 1.0, A.is_equal)
+        tt(vw("pq"), vw("on1"), vw("pQ", 0, 128), A.mult)
+        scan(vw("sq"), vw("d0s"), vw("pq"), A.mult, A.add)
+        for w in range(8):
+            ts(vw("dg", 128 * w, 128 * w + 128), vw("I16"), vw("sq", 16 * w + 15, 16 * w + 16), A.mult)
+
+    def spread():
+        for b, p in ((0, "pD"), (1, "pT")):
+            mm(vw(p), vw("Ib"), vw("tri"), True, False)
+            mm(vw(p), vw("on16"), vw("dg", 512 * b, 512 * b + 512), False, True)
+
+    def equal():
+        for w in range(8):
+            p = vw("pD" if w < 4 else "pT", 128 * (w % 4), 128 * (w % 4) + 128)
+            ts(vw("eq", 128 * w, 128 * w + 128), p, vw("sq", 16 * w + 15, 16 * w + 16), A.is_equal)
 
     def dedupe():
-        for b in (0, 1):
-            for w in range(4 * b, 4 * b + 4):
-                ts(vw("dg", 128 * w, 128 * w + 128), vw("I16"), vw("sq", 16 * w + 15, 16 * w + 16), A.mult)
-            mm(vw("pD"), vw("I16"), vw("tri"), True, False)
-            mm(vw("pD"), vw("on16"), vw("dg", 512 * b, 512 * b + 512), False, True)
-            for w in range(4 * b, 4 * b + 4):
-                ts(vw("eq", 128 * w, 128 * w + 128), vw("pD", 128 * (w - 4 * b), 128 * (w - 4 * b) + 128), vw("sq", 16 * w + 15, 16 * w + 16), A.is_equal)
-        for w in range(8):
-            mm(vw("pL", 272 + w, 273 + w), vw("eq", 128 * w, 128 * w + 128), vw("on", 0, 1))
         ts(vw("du"), vw("pL", 272, 280), 0.5, A.is_lt)
         tt(vw("uu"), vw("du"), vw("sq", 15, 128, 16), A.mult)
         ts(vw("ut"), vw("uu"), 0.0, A.is_equal, vw("dum"), A.mult)
@@ -395,11 +402,21 @@ def member(g, core, rank, T, topo):
             ts(vw("AS", 16 * w, 16 * w + 16), vw("m16"), vw("of", w, w + 1), A.mult)
         mm(vw("pL", 264, 272), vw("AS"), vw("bo8h"))
         copy(vw("ls"), vw("pL", 264, 272))
+
+    def update():
         tt(vw("xs"), ind(vw("X"), vw("ls")), vw("ti"), A.add)
         ts(vw("xn"), vw("xs"), 0.5, A.mult, -0.25, A.add)
 
     def scatter():
         copy(ind(vw("X"), vw("ls")), vw("xn"))
+
+    def sums():
+        for m in range(16):
+            mm(vw("pT", 0, 128), vw("Ib"), vw("x", m, 2048, 16), m == 0, False)
+        mm(vw("pT", 0, 128), vw("bo"), vw("eR"), False, True)
+
+    def tsixteenth():
+        ts(vw("ti"), vw("pT", 0, 128), 0.0625, A.mult, -0.46875, A.add)
 
     def stops():
         mm(vw("pT", 128, 136), vw("on32"), vw("stp"))
@@ -408,6 +425,10 @@ def member(g, core, rank, T, topo):
         copy(vw("ci"), vw("cn"))
         ts(vw("cj"), vw("ci"), 255, A.bitwise_and)
         copy(vw("c16"), vw("cj"))
+
+    def rowsums(h):
+        for m in range(16):
+            mm(vw("pW", m, 128, 16, *HV[h]), vw("x", 1024 * h + m, 1024 * h + 1024, 16), vw("bo8"))
 
     for t in range(VI):
         q, v = "q%d" % t, "v%d" % t
@@ -419,23 +440,33 @@ def member(g, core, rank, T, topo):
                 recs.setdefault("%s%d" % (k, t), []).append((vw("%s%d" % (k, t), *HV[h]), True, (s, 8), "remote"))
             xgath("v", "x", q, 0, 32)
             xgath("s", "x", q, 32, 64)
+        ts(vw("eR"), vw(q), 0, A.is_equal)
+        if t:
             xgath("v", "x", q, 64, 96)
             xgath("s", "x", q, 96, 128)
-        ts(vw("eR"), vw(q), 0, A.is_equal)
+        rowsums(0)
+        mm(vw("pT", 256, 264), vw("eR"), vw("bo8"))
+        rowsums(1)
         ts(vw("q16"), vw(q), 0.0, A.add)
+        mm(vw("pQ", 0, 128), vw("q16"), vw("I16"))
+        if t:
+            ts(vw("n1"), vw("pT", 256, 264), -16.0, A.mult, vw("c16"), A.add)
+        else:
+            mm(vw("pT", 264, 272), vw("on32"), vw("lim8"))
+            copy(vw("limb"), vw("pT", 264, 272))
+            ts(vw("n1"), vw("pT", 256, 264), -16.0, A.mult)
+        ts(vw("n0"), vw("pT", 256, 264), 0.0, A.is_equal, -4194304.0, A.mult)
+        tt(vw("n2"), vw("n1"), vw("limb"), A.add)
+        tt(vw("thr"), vw("n2"), vw("n0"), A.add)
         if t:
             ts(vw("aa"), vw(v), 65535, A.bitwise_and)
             copy(vw("aF"), vw("aa"))
-        for c in range(4):
+            mm(vw("pA", 0, 128), vw("aF"), vw("I32"))
+        else:
             for m in range(16):
-                mm(vw("pW", m, 128, 16, 32 * c, 32 * c + 32), vw("x", 512 * c + m, 512 * c + 512, 16), vw("bo8"))
-        mm(vw("pT", 256, 264), vw("eR"), vw("bo8"))
-        ts(vw("n0"), vw("pT", 256, 264), 0.0, A.is_equal, -4194304.0, A.mult)
-        ts(vw("n1"), vw("pT", 256, 264), -16.0, A.mult, vw("c16") if t else 0.0, A.add)
-        tt(vw("n2"), vw("n1"), vw("limb"), A.add)
-        tt(vw("thr"), vw("n2"), vw("n0"), A.add)
-        mm(vw("pA", 0, 128), vw("aF"), vw("I32"))
-        mm(vw("pQ", 0, 128), vw("q16"), vw("I16"))
+                mm(vw("pA", m, 128, 16), vw("CB", m, 2048, 16), vw("bo8b"))
+        if t == VI - 1:
+            sums()
         key = vw("pW", 0, 128)
         scan(vw("sm"), vw("d0s"), key, A.mult, A.add)
         scan(vw("mx"), vw("d0m"), key, A.add, A.max)
@@ -450,13 +481,10 @@ def member(g, core, rank, T, topo):
         mm(vw("pL", 384, 512), vw("q2P"), vw("I16"))
         copy(vw("q2u"), vw("pL", 384, 512))
         xgath("s", "x2", "q2u", 64, 128, True)
+        ts(vw("e2"), vw("q2u"), 0, A.is_equal)
         xgath("v", "x2", "q2u", 0, 64, True)
         if t == 0:
             late_constants()
-        ts(vw("e2"), vw("q2u"), 0, A.is_equal)
-        for m in range(16):
-            mm(vw("pT", 0, 128), vw("Ib"), vw("x", m, 2048, 16), m == 0, False)
-        mm(vw("pT", 0, 128), vw("bo"), vw("eR"), False, True)
         mm(vw("pL", 0, 128), vw("e2"), vw("cm"))
         mm(vw("pL", 128, 256), vw("cm"), vw("e2"))
         scan(vw("bs", 0, 1024), vw("d0b", 0, 1024), vw("x2", 0, 1024), A.add, A.max)
@@ -472,14 +500,11 @@ def member(g, core, rank, T, topo):
         mm(ku, vw("lo"), vw("Im16"), False, True)
         ts(vw("eP"), vw("pL", 0, 128), -16.5, A.is_lt)
         ts(vw("eQ"), vw("pL", 128, 256), -16.5, A.is_lt)
-        ts(vw("q2h"), vw("q2u"), 0.0, A.add)
-        ts(vw("fR"), vw("q2u"), 0, A.is_gt)
-        tt(vw("vv"), vw(v), vw("fR"), A.mult)
-        ts(vw("aM"), vw("aF"), vw("m64"), A.add)
-        ts(vw("ti"), vw("pT", 0, 128), 0.0625, A.mult, -0.46875, A.add)
-        ts(vw("on1"), vw("pw"), 1.0, A.is_equal)
-        tt(vw("pq"), vw("on1"), vw("pQ", 0, 128), A.mult)
-        scan(vw("sq"), vw("d0s"), vw("pq"), A.mult, A.add)
+        if t == VI - 1:
+            tsixteenth()
+        stopped()
+        if t == 0:
+            act(vw("aP0"), vw("pA", 0, 128))
         ts(vw("u1"), ku, 1.0 / 4096, A.mult, 1156.5 + 1.0 / 8192, A.add)
         mm(vw("pS", 128, 256), vw("u1"), vw("I16"))
         for j in range(16):
@@ -497,27 +522,32 @@ def member(g, core, rank, T, topo):
         mm(vw("pL", 256, 264), vw("AL"), vw("bo8h"))
         copy(vw("lk"), vw("pL", 256, 264))
         copy(vw("cd"), ind(vw("R"), vw("lk")))
-        xgath("s", "xc", "cd", 0, 128, False, 16)
+        spread()
         mm(vw("pA", 256, 384), vw("ok"), vw("I16"))
-        if t == VI - 1:
-            dedupe()
-        for c in range(4):
-            tt(vw("mn", 512 * c, 512 * c + 512), ind(vw("X", 16, 16 + D), vw("cd", 32 * c, 32 * c + 32)), vw("vf", 512 * c, 512 * c + 512), A.min)
-            if c == 0:
-                tt(vw("oka"), vw("pA", 256, 384), vw("aM"), A.mult)
-                ts(vw("cd16"), vw("cd"), 16.0, A.add)
+        if t == 0:
+            mm(vw("pA", 384, 512), vw("aP0"), vw("I32"))
+        for a, b in ((0, 64), (64, 96), (96, 128)):
+            d = vw("mn", 16 * a, 16 * b)
+            tt(d, ind(vw("X", 16, 16 + D), vw("cd", a, b)), vw("vf", 16 * a, 16 * b), A.subtract)
+            act(vw("xc", 16 * a, 16 * b), d, 1.0, 0.0, F.Abs)
+            for j in range(16):
+                mm(vw("pS", j, 128, 16, a, b), vw("xc", 16 * a + j, 16 * b, 16), vw("wm16"))
+        if t == 0:
+            tt(vw("aF"), vw("pA", 384, 512), vw("fil"), A.mult)
+            ts(vw("w0"), vw("wy0"), 65536.0, A.mult)
+            tt(vw("v0"), vw("aF"), vw("w0"), A.add)
+        ts(vw("aM"), vw("aF"), vw("m64"), A.add)
+        tt(vw("oka"), vw("pA", 256, 384), vw("aM"), A.mult)
+        ts(vw("cd16"), vw("cd"), 16.0, A.add)
+        ts(vw("fR"), vw("q2u"), 0, A.is_gt)
+        tt(vw("vv"), vw(v), vw("fR"), A.mult)
+        ts(vw("q2h"), vw("q2u"), 0.0, A.add)
+        equal()
+        mm(vw("pQ", 128, 256), vw("cd16"), vw("I16"))
+        for w in range(8):
+            mm(vw("pL", 272 + w, 273 + w), vw("eq", 128 * w, 128 * w + 128), vw("on", 0, 1))
         mm(vw("pA", 128, 256), vw("bo32"), vw("oka"), True, False)
         mm(vw("pA", 128, 256), vw("I32"), vw("bit"), False, True)
-        mm(vw("pQ", 128, 256), vw("cd16"), vw("I16"))
-        for j in range(16):
-            mm(vw("pW", 256 + j, 384, 16), vw("xc", j, 2048, 16), vw("wm16"))
-        tt(vw("xk"), vw("pW", 256, 384), vw("tief"), A.add)
-        for c in range(4):
-            for j in range(16):
-                mm(vw("pS", j, 128, 16, 32 * c, 32 * c + 32), vw("mn", 512 * c + j, 512 * c + 512, 16), vw("w32"))
-        tt(vw("t3"), vw("pA", 128, 256), vw("eQ"), A.mult)
-        vo = "vo%d" % (t + 1) if t < VI - 1 else "vI"
-        tt(vw(vo), vw("vv"), vw("t3"), A.add)
 
         def send(k):
             src = "%so%d" % (k, t + 1)
@@ -532,15 +562,12 @@ def member(g, core, rank, T, topo):
             deps("g", [], [vw(src)])
             g.remote_dma_fused(tr, local_sem=T.sem["loc"])
             cnt["loc"] = cnt.get("loc", 0) + 16
-        if t < VI - 1:
-            send("v")
         if t == VI - 1:
+            dedupe()
+            update()
             scatter()
             store(T.yx[:, :], vw("X", 16, 16 + D), "st0")
-            ts(vw("bb"), vw("vI"), 16, A.arith_shift_right)
-            copy(vw("yw"), vw("bb"))
-            store(T.yq[:, :], vw("yw"), "st1")
-        tt(vw("ky"), vw("pS", 0, 128), vw("xk"), A.add)
+        tt(vw("ky"), vw("pS", 0, 128), vw("tief"), A.add)
         scan(vw("ms"), vw("d0m"), vw("ky"), A.add, A.max)
         for w in range(8):
             ts(vw("oj", 16 * w, 16 * w + 16), vw("ky", 16 * w, 16 * w + 16), vw("ms", 16 * w + 15, 16 * w + 16), A.is_equal)
@@ -554,14 +581,25 @@ def member(g, core, rank, T, topo):
         if t < VI - 1:
             copy(vw("qo%d" % (t + 1)), nq)
             send("q")
-            stops()
-            dedupe()
-            scatter()
         else:
-            ts(vw("yt"), nq, 0.0, A.is_equal, float(16 + D), A.mult)
-            tt(vw("yo"), vw("yt"), nq, A.add)
+            ts(vw("yo"), nq, 0.0, A.is_equal, float(16 + D), A.mult)
+            tt(vw("yo"), vw("yo"), nq, A.add)
             ts(vw("yt"), vw("yo"), -16.0, A.add)
             store(T.yp[:, :], vw("yt"), "st2")
+        tt(vw("t3"), vw("pA", 128, 256), vw("eQ"), A.mult)
+        tt(vw("vo%d" % (t + 1) if t < VI - 1 else "vI"), vw("vv"), vw("t3"), A.add)
+        if t < VI - 1:
+            send("v")
+            sums()
+            dedupe()
+            stops()
+            tsixteenth()
+            update()
+            scatter()
+        else:
+            ts(vw("bb"), vw("vI"), 16, A.arith_shift_right)
+            copy(vw("yw"), vw("bb"))
+            store(T.yq[:, :], vw("yw"), "st1")
     for s in SEMAPHORES:
         if cnt.get(s):
             g.wait_ge(T.sem[s], cnt[s])

import numpy as np
from concourse.bass import DstId, RemoteDMATransfer, IndirectOffsetOnAxis
from concourse.mybir import dt, AluOpType, AxisListType, ActivationFunctionType

A = AluOpType
F = ActivationFunctionType
NR, VI, H, L, D = 8, 4, 64, 128, 1760
STRIDE = (4, 1)
XW = 16 + D + 128
f32, b16, h16, i32, u16 = "float32", "bfloat16", "float16", "int32", "uint16"
SB = {
    "X": (XW, b16), "R": (16 + D, i32), "dr0": (L, i32), "wy0": (L, i32), "lmI": (1, i32),
    "kI": (1, i32), "aI": (1, i32), "gI": (1, i32), "kc": (1, f32), "ac": (1, f32), "gc": (1, f32),
    "cid": (128, f32), "mro": (128, f32), "g8": (8, f32), "j16": (16, f32),
    "I32": (128, f32), "I16": (128, h16), "Ib": (128, b16), "I16b": (128, b16), "Im16": (128, h16),
    "bo": (128, b16), "bo32": (128, f32), "bo256": (128, b16),
    "bo8": (8, b16), "bo8h": (8, h16), "wm16": (8, b16), "w32": (8, b16), "bo8a": (8, b16), "bo8b": (8, b16),
    "on": (128, b16), "on32": (128, f32), "on16": (128, h16), "tie16": (128, b16), "tief": (128, f32),
    "m15": (16, f32), "m16": (16, h16), "cm": (128, b16), "d0m": (128, f32), "d0s": (128, f32), "d0p": (128, f32), "d0b": (2048, b16),
    "pw2": (16, f32), "one16": (16, f32), "pwo": (16, f32), "m64": (1, f32), "dum": (1, f32),
    "bit": (128, f32), "tri": (512, b16), "limb": (8, f32), "limf": (1, f32), "lim8": (8, f32),
    "pofI": (128, i32), "pof16": (128, h16),
    "IF": (1024, b16), "IG": (1024, b16), "PA": (2048, b16), "PB": (2048, b16), "CA": (2048, b16), "CB": (2048, b16),
    "LW": (2048, b16), "lf": (128, f32), "lu1": (128, u16), "lu2": (128, u16), "lu4": (128, u16), "lu8": (128, u16),
    "qf0": (128, f32), "fil": (128, f32), "aP0": (128, f32), "w0": (128, f32),
    "x": (2048, b16), "x2": (2048, b16), "xc": (2048, b16), "mn": (2048, b16), "vf": (2048, b16), "bs": (2048, h16),
    "eR": (128, b16), "e2": (128, b16), "q16": (128, h16), "aa": (128, i32), "aF": (128, f32), "aM": (128, f32),
    "n0": (8, f32), "n1": (8, f32), "n2": (8, f32), "thr": (8, f32), "mx": (128, f32), "sm": (128, f32), "stp": (8, f32),
    "oh": (128, f32), "pw": (128, f32), "pr": (128, i32), "bb": (128, i32), "q2P": (128, h16), "q2u": (128, u16), "q2h": (128, h16),
    "fR": (128, b16), "vv": (128, f32), "lo": (128, h16), "u1": (128, h16), "eP": (128, f32), "eQ": (128, f32),
    "mk": (128, f32), "zi": (8, i32), "r16": (8, f32), "ok": (128, h16), "pk": (128, f32), "sk": (128, f32), "AL": (128, h16), "lk": (8, u16),
    "cd": (128, u16), "cd16": (128, h16), "oka": (128, f32), "t3": (128, f32), "xk": (128, f32), "ky": (128, f32),
    "ms": (128, f32), "oj": (128, f32), "pn": (128, f32), "sn": (128, f32), "AN": (128, h16),
    "on1": (128, f32), "pq": (128, f32), "sq": (128, f32), "dg": (1024, h16), "eq": (1024, b16), "du": (8, f32), "uu": (8, f32), "ut": (8, f32), "of": (8, f32), "AS": (128, h16), "ls": (8, u16),
    "ti": (128, i32), "xs": (128, f32), "xn": (128, i32), "cn": (1, f32), "ci": (1, i32), "cj": (1, i32), "c16": (1, f32),
    "yt": (128, f32), "yo": (128, f32), "vI": (128, i32), "yw": (128, f32),
}
ALONE = ("X", "R", "dr0", "wy0", "lmI", "yt", "yw", "IF", "IG")
ALIAS, SCRATCH, _wide = {}, {}, {}
for _k, (_w, _d) in SB.items():
    if _w > 1024 or _k in ALONE:
        SCRATCH[_k] = ("sbuf", [128, _w], _d)
    else:
        ALIAS[_k] = ("p_" + _d, _wide.get(_d, 0))
        _wide[_d] = _wide.get(_d, 0) + -(-_w // 16) * 16
for _d, _w in _wide.items():
    SCRATCH["p_" + _d] = ("sbuf", [128, _w], _d)
for _t in range(VI):
    SCRATCH["q%d" % _t] = ("sbuf", [128, L], u16)
    SCRATCH["v%d" % _t] = ("sbuf", [128, L], i32)
for _t in range(1, VI):
    SCRATCH["qo%d" % _t] = ("sbuf", [128, L], u16)
    SCRATCH["vo%d" % _t] = ("sbuf", [128, L], i32)
    SCRATCH["rq%d" % _t] = ("sbuf", [128, H], u16)
    SCRATCH["rv%d" % _t] = ("sbuf", [128, H], i32)
PS = ("pW", "pT", "pU", "pS", "pQ", "pA", "pL", "pD")
for _p in PS:
    SCRATCH[_p] = ("psum", [128, 512], f32)
SEMAPHORES = ["ev", "es", "et", "eg", "loc"] + ["ld%d" % _t for _t in range(5)] + ["st%d" % _t for _t in range(3)]
for _t in range(1, VI):
    SEMAPHORES += ["%s%d" % (_n, _t) for _n in ("qL", "qH", "vL", "vH", "rq", "rv")]
HV = ((0, 64), (64, 128))


def relay_of(core, dst, topo):
    c = [k for k in topo.cores_of(core) if k != core and topo.may_write(k, dst)]
    return ([k for k in c if topo.die(k) == topo.die(core)] + c)[0]


def bits(topo, src, dst, n, top):
    e = topo.engines(src, dst)
    e = e[len(e) - n:] if top else e[:n]
    return sum(1 << k for k in e)


def rank_program(g, core, T, topo):
    rank = T.rank_of(core)
    if rank is None:
        for r, c in enumerate(T.cores):
            dst = T.cores[(r + STRIDE[1]) % NR]
            if relay_of(c, dst, topo) == core:
                relay(g, core, dst, T, topo)
        return
    member(g, core, rank, T, topo)


def relay(g, core, dst, T, topo):
    rid, pid = topo.addr(dst, core)
    m = bits(topo, core, dst, 8, False)
    n = 0
    for t in range(1, VI):
        for k in ("q", "v"):
            g.wait_ge(T.sem["r%s%d" % (k, t)], 8)
            g.remote_dma(T["%s%d" % (k, t)][:, H:L], T["r%s%d" % (k, t)][:, :], T.sem["%sH%d" % (k, t)], T.sem["loc"], pid, rid, m)
            n += 8
    g.wait_ge(T.sem["loc"], n)


def member(g, core, rank, T, topo):
    Q = {"v": g.vector, "s": g.scalar, "t": g.tensor, "g": g, "y": g.sync}
    ES = {"v": "ev", "s": "es", "t": "et", "g": "eg"}
    cnt = {}
    known = {q: {} for q in Q}
    snap = {}
    recs = {}
    psum = set(PS)

    def vw(name, lo=0, hi=None, st=1, r0=0, r1=128):
        if hi is None:
            hi = SB[name][0] if name in SB else SCRATCH[name][1][1]
        if name in ALIAS:
            name, o = ALIAS[name]
            lo, hi = lo + o, hi + o
        ap = T[name][r0:r1, lo:hi:st] if st > 1 else T[name][r0:r1, lo:hi]
        return {"ap": ap, "n": name, "lo": lo, "hi": hi, "st": st, "x": None}

    def ind(w, o):
        return {"ap": w["ap"].indirect(o["ap"]), "n": w["n"], "lo": w["lo"], "hi": w["hi"], "st": 1, "x": o}

    def clash(a, b):
        if a["n"] in psum:
            return True
        if a["lo"] >= b["hi"] or b["lo"] >= a["hi"]:
            return False
        return not (a["st"] > 1 and a["st"] == b["st"] and (a["lo"] - b["lo"]) % a["st"])

    def need(q, tok):
        s, n = tok
        if known[q].get(s, 0) >= n:
            return
        Q[q].wait_ge(T.sem[s], n)
        known[q][s] = n
        for k, m in snap.get(tok, {}).items():
            if known[q].get(k, 0) < m:
                known[q][k] = m

    def expand(vs):
        r = []
        for a in vs:
            if isinstance(a, dict):
                r.append(a)
                if a["x"]:
                    r.append(a["x"])
        return r

    def deps(q, outs, ins):
        best = {}
        for a, wr in [(a, True) for a in outs] + [(a, False) for a in ins]:
            for b, bw, tok, bq in recs.get(a["n"], []):
                if not clash(a, b):
                    continue
                if a["n"] in psum:
                    over = not (a["lo"] >= b["hi"] or b["lo"] >= a["hi"])
                    if bq == q and (q == "t" or not (over and bw and not wr)):
                        continue
                else:
                    if not wr and not bw:
                        continue
                    if bq == q and q != "y" and not bw:
                        continue
                best[tok[0]] = max(best.get(tok[0], 0), tok[1])
        for s in sorted(best):
            need(q, (s, best[s]))

    def note(q, tok, outs, ins):
        for a, wr in [(a, True) for a in outs] + [(a, False) for a in ins]:
            l = recs.setdefault(a["n"], [])
            if wr and a["st"] == 1 and a["n"] not in psum:
                l[:] = [b for b in l if not (a["lo"] <= b[0]["lo"] and b[0]["hi"] <= a["hi"])]
            elif a["n"] in psum or not wr:
                l[:] = [b for b in l if not (b[3] == q and b[1] == wr and b[0]["lo"] == a["lo"] and b[0]["hi"] == a["hi"] and b[0]["st"] == a["st"])]
            l.append((a, wr, tok, q))

    def op(q, outs, ins, fn, sem=None, inc=1):
        ins = expand(ins + [a["x"] for a in outs])
        deps(q, outs, ins)
        s = sem or ES[q]
        fn().then_inc(T.sem[s], inc)
        cnt[s] = cnt.get(s, 0) + inc
        tok = (s, cnt[s])
        snap[tok] = dict(known[q])
        note(q, tok, outs, ins)

    def P(a):
        return a["ap"] if isinstance(a, dict) else a

    def copy(o, i):
        op("v", [o], [i], lambda: g.vector.tensor_copy(P(o), P(i)))

    def tt(o, a, b, f):
        op("v", [o], [a, b], lambda: g.vector.tensor_tensor(P(o), P(a), P(b), f))

    def ts(o, a, s1, f1, s2=None, f2=None):
        if s2 is None:
            op("v", [o], [a, s1], lambda: g.vector.tensor_scalar(P(o), P(a), P(s1), None, f1))
        else:
            op("v", [o], [a, s1, s2], lambda: g.vector.tensor_scalar(P(o), P(a), P(s1), P(s2), f1, f2))

    def scan(o, d0, d1, f0, f1, init=0.0):
        op("v", [o], [d0, d1], lambda: g.vector.tensor_tensor_scan(P(o), P(d0), P(d1), init, f0, f1))

    def fill(o, c):
        op("v", [o], [], lambda: g.vector.memset(P(o), c))

    def act(o, i, scale=1.0, bias=0.0, func=F.Identity):
        op("s", [o], [i, scale], lambda: g.scalar.activation(P(o), P(i), func, bias=bias, scale=P(scale)))

    def mm(o, a, b, start=True, stop=True):
        op("t", [o], [a, b], lambda: g.tensor.matmul(P(o), P(a), P(b), start, stop))

    def load(o, src, sem, q="y"):
        op(q, [o], [], lambda: Q[q].dma_start(P(o), src), sem, 16)

    def store(dst, i, sem, q="y"):
        op(q, [], [i], lambda: Q[q].dma_start(dst, P(i)), sem, 16)

    def iota(o, pat, base, cm, fl=True):
        op("g", [o], [], lambda: g.iota(P(o), pat, base, cm, allow_small_or_imprecise_dtypes=True) if fl else g.iota(P(o), pat, base, cm))

    def gfill(o, n, c, fl=True):
        iota(o, [[0, n]], c, 0, fl)

    def sel(o, pat, f, c, base, cm):
        op("g", [o], [o], lambda: g.affine_select(P(o), P(o), pat, f, c, base, cm))

    def half(name, h):
        return vw(name, 1024 * h, 1024 * h + 1024)

    load(vw("wy0"), T.why[:, :], "ld0")
    load(vw("dr0"), T.drugs[:, :], "ld1", "s")
    load(vw("X", 16, 16 + D), T.eff[:, :], "ld2")
    load(vw("lmI"), T.lim[:, :], "ld3", "s")
    load(vw("R", 16, 16 + D), T.rem[:, :], "ld4")
    iota(vw("kI"), [[1, 1]], 0, 1, False)
    iota(vw("mro"), [[0, 8], [1, 16]], 0, 0)
    iota(vw("pofI"), [[0, 2], [16, 64]], 0, 0, False)
    iota(vw("g8"), [[1, 8]], 0, 0)
    iota(vw("cid"), [[1, 128]], 0, 0)
    iota(vw("j16"), [[1, 16]], 0, 0)
    fill(vw("LW"), 0.0)
    ts(vw("aI"), vw("kI"), 15, A.bitwise_and)
    copy(vw("ac"), vw("aI"))
    ts(vw("IF", 0, 128), vw("mro"), vw("ac"), A.is_equal)
    for h in (128, 256, 512):
        copy(vw("IF", h, 2 * h), vw("IF", 0, h))
    act(vw("IG"), vw("IF"))
    ts(vw("gI"), vw("kI"), 4, A.arith_shift_right)
    copy(vw("gc"), vw("gI"))
    copy(vw("kc"), vw("kI"))
    ts(vw("bo8"), vw("g8"), vw("gc"), A.is_equal)
    ts(vw("bo8a"), vw("bo8"), vw("ac"), A.mult)
    tt(vw("lf"), vw("wy0"), vw("pofI"), A.add)
    copy(vw("lu1"), vw("lf"))

    def win(name, h):
        return vw("IF") if name == "IF" else half(name, h)

    def pgath(q, dst, src, lst, h):
        o, w, f = half(dst, h), win(src, h), vw(lst, *HV[h])
        if q == "s":
            act(o, ind(w, f))
        else:
            copy(o, ind(w, f))

    def cgath(dst, src, lst, h, by=None):
        o, w, f = half(dst, h), win(src, h), vw(lst, *HV[h])
        d = vw("IG") if src == "IF" else half("xc", h)
        if by == "s":
            act(d, w)
        elif by == "v":
            copy(d, w)
        tt(o, ind(w, f), d, A.max)

    def xgath(q, dst, lst, c0, c1, conv=False, lo=0):
        o, w, f = vw(dst, 16 * c0, 16 * c1), vw("X", lo, 16 + D), vw(lst, c0, c1)
        if q == "s":
            act(o, ind(w, f), 16.0, -2048.0) if conv else act(o, ind(w, f))
        elif conv:
            ts(o, ind(w, f), 16.0, A.mult, -2048.0, A.add)
        else:
            copy(o, ind(w, f))

    def conv(src, h):
        o = vw("pU" if h == 0 else "pS", 0, 64)
        mm(o, vw("I16"), vw("pof16", *HV[h]), True, False)
        for m in range(16):
            mm(o, vw("LW", 128 * m, 128 * m + 128), vw(src, 1024 * h + m, 1024 * h + 1024, 16), False, m == 15)

    def convd(lst, h):
        copy(vw(lst, *HV[h]), vw("pU" if h == 0 else "pS", 0, 64))
    pgath("s", "PA", "IF", "lu1", 0)
    pgath("v", "PA", "IF", "lu1", 1)
    for m in range(16):
        o = vw("LW", 128 * m + m, 128 * m + 128, 16)
        act(o, vw("bo8a")) if m % 4 else copy(o, vw("bo8a"))
    pgath("s", "PB", "PA", "lu1", 0)
    ts(vw("I32"), vw("cid"), vw("kc"), A.is_equal)
    copy(vw("I16"), vw("I32"))
    copy(vw("pof16"), vw("pofI"))
    pgath("v", "PB", "PA", "lu1", 1)
    conv("PB", 0)
    conv("PB", 1)
    gfill(vw("X", 0, 16), 16, -1)
    gfill(vw("X", 16 + D, XW), 128, 0)
    gfill(vw("R", 0, 16), 16, 0, False)
    gfill(vw("d0b"), 2048, 1)
    sel(vw("d0b"), [[0, 128], [1, 16]], A.not_equal, -8192.0, 0, 0)
    for n, c, z in (("d0s", 1, 0.0), ("d0m", 0, -16777216.0), ("d0p", 2, 0.0)):
        gfill(vw(n), 128, c)
        sel(vw(n), [[0, 8], [1, 16]], A.not_equal, z, 0, 0)
    gfill(vw("on32"), 128, 1)
    gfill(vw("on"), 128, 1)
    gfill(vw("bo32"), 128, 1)
    gfill(vw("cm"), 128, 65)
    sel(vw("cm"), [[1, 128]], A.is_gt, 1.0, 0, -1)
    sel(vw("cm"), [[1, 128]], A.not_equal, -31.0, 0, -1)
    for n in ("bo32", "cm"):
        sel(vw(n), [[-16, 8], [0, 16]], A.is_ge, 0.0, 0, 1)
        sel(vw(n), [[16, 8], [0, 16]], A.is_ge, 0.0, 15, -1)
    gfill(vw("tri"), 512, 4096)
    sel(vw("tri"), [[0, 4], [-1, 128]], A.is_ge, 0.0, 0, 1)
    cgath("CA", "IF", "lu1", 0)
    convd("lu2", 0)
    pgath("s", "mn", "PB", "lu2", 0)
    conv("mn", 0)
    convd("lu2", 1)
    cgath("CA", "IF", "lu1", 1)
    ts(vw("fil"), vw("dr0"), D, A.is_lt)
    ts(vw("qf0"), vw("dr0"), 16, A.add)
    tt(vw("qf0"), vw("qf0"), vw("fil"), A.mult)
    copy(vw("q0"), vw("qf0"))
    pgath("s", "mn", "PB", "lu2", 1)
    conv("mn", 1)
    cgath("CB", "CA", "lu2", 0, "v")
    convd("lu4", 0)
    act(half("xc", 1), half("CA", 1))
    pgath("s", "PB", "mn", "lu4", 0)
    conv("PB", 0)
    cgath("CB", "CA", "lu2", 1)
    convd("lu4", 1)
    pgath("s", "PB", "mn", "lu4", 1)
    conv("PB", 1)
    xgath("s", "x", "q0", 0, 64)
    ts(vw("pw2"), vw("j16"), vw("ac"), A.is_lt, 1.0, A.add)
    fill(vw("one16"), 1.0)
    scan(vw("pwo"), vw("pw2"), vw("one16"), A.mult, A.mult, 1.0)
    pcol = vw("pwo", 15, 16)
    ts(vw("bo8b"), vw("bo8"), pcol, A.mult)
    cgath("CA", "CB", "lu4", 0, "v")
    convd("lu8", 0)
    act(half("xc", 0), half("CA", 0))
    cgath("CA", "CB", "lu4", 1, "v")
    convd("lu8", 1)
    act(half("xc", 1), half("CA", 1))
    xgath("s", "x", "q0", 64, 128)
    act(vw("Ib"), vw("I32"))
    act(vw("wm16"), vw("bo8"), -16.0)
    act(vw("w32"), vw("bo8"), 32.0)
    act(vw("bo"), vw("bo32"))
    act(vw("I16b"), vw("I32"), 16.0)
    act(vw("bo256"), vw("bo32"), 256.0)
    act(vw("tie16"), vw("mro"), -16.0, 240.0)
    act(vw("tief"), vw("mro"), -1.0, 15.0)
    act(vw("m15"), vw("mro", 0, 16), -1.0, 15.0)
    act(vw("bit"), vw("on32"), pcol)
    copy(vw("limf"), vw("lmI"))
    ts(vw("lim8"), vw("I32", 0, 128, 16), vw("limf"), A.mult)
    cgath("CB", "CA", "lu8", 0)
    cgath("CB", "CA", "lu8", 1)

    def late_constants():
        fill(vw("on16"), 1.0)
        ts(vw("Im16"), vw("I32"), -16.0, A.mult)
        copy(vw("bo8h"), vw("bo8"))
        copy(vw("m16"), vw("IF", 0, 16))
        ts(vw("m64"), vw("ac"), 65536.0, A.mult)
        ts(vw("dum"), vw("kc"), float(16 + D), A.add)

    def stopped():
        ts(vw("on1"), vw("pw"), 1.0, A.is_equal)
        tt(vw("pq"), vw("on1"), vw("pQ", 0, 128), A.mult)
        scan(vw("sq"), vw("d0s"), vw("pq"), A.mult, A.add)
        for w in range(8):
            ts(vw("dg", 128 * w, 128 * w + 128), vw("I16"), vw("sq", 16 * w + 15, 16 * w + 16), A.mult)

    def spread():
        for b, p in ((0, "pD"), (1, "pT")):
            mm(vw(p), vw("Ib"), vw("tri"), True, False)
            mm(vw(p), vw("on16"), vw("dg", 512 * b, 512 * b + 512), False, True)

    def equal():
        for w in range(8):
            p = vw("pD" if w < 4 else "pT", 128 * (w % 4), 128 * (w % 4) + 128)
            ts(vw("eq", 128 * w, 128 * w + 128), p, vw("sq", 16 * w + 15, 16 * w + 16), A.is_equal)

    def dedupe():
        ts(vw("du"), vw("pL", 272, 280), 0.5, A.is_lt)
        tt(vw("uu"), vw("du"), vw("sq", 15, 128, 16), A.mult)
        ts(vw("ut"), vw("uu"), 0.0, A.is_equal, vw("dum"), A.mult)
        tt(vw("of"), vw("uu"), vw("ut"), A.add)
        for w in range(8):
            ts(vw("AS", 16 * w, 16 * w + 16), vw("m16"), vw("of", w, w + 1), A.mult)
        mm(vw("pL", 264, 272), vw("AS"), vw("bo8h"))
        copy(vw("ls"), vw("pL", 264, 272))

    def update():
        tt(vw("xs"), ind(vw("X"), vw("ls")), vw("ti"), A.add)
        ts(vw("xn"), vw("xs"), 0.5, A.mult, -0.25, A.add)

    def scatter():
        copy(ind(vw("X"), vw("ls")), vw("xn"))

    def sums():
        for m in range(16):
            mm(vw("pT", 0, 128), vw("Ib"), vw("x", m, 2048, 16), m == 0, False)
        mm(vw("pT", 0, 128), vw("bo"), vw("eR"), False, True)

    def tsixteenth():
        ts(vw("ti"), vw("pT", 0, 128), 0.0625, A.mult, -0.46875, A.add)

    def stops():
        mm(vw("pT", 128, 136), vw("on32"), vw("stp"))
        o, i = vw("cn"), vw("pT", 128, 136)
        op("v", [o], [i], lambda: g.vector.tensor_reduce(P(o), P(i), AxisListType.X, A.add))
        copy(vw("ci"), vw("cn"))
        ts(vw("cj"), vw("ci"), 255, A.bitwise_and)
        copy(vw("c16"), vw("cj"))

    def rowsums(h):
        for m in range(16):
            mm(vw("pW", m, 128, 16, *HV[h]), vw("x", 1024 * h + m, 1024 * h + 1024, 16), vw("bo8"))

    for t in range(VI):
        q, v = "q%d" % t, "v%d" % t
        if t:
            for k, h in (("q", 0), ("v", 0), ("q", 1), ("v", 1)):
                s = "%s%s%d" % (k, "LH"[h], t)
                cnt[s] = 8
                snap[(s, 8)] = {}
                recs.setdefault("%s%d" % (k, t), []).append((vw("%s%d" % (k, t), *HV[h]), True, (s, 8), "remote"))
            xgath("v", "x", q, 0, 32)
            xgath("s", "x", q, 32, 64)
        ts(vw("eR"), vw(q), 0, A.is_equal)
        if t:
            xgath("v", "x", q, 64, 96)
            xgath("s", "x", q, 96, 128)
        rowsums(0)
        mm(vw("pT", 256, 264), vw("eR"), vw("bo8"))
        rowsums(1)
        ts(vw("q16"), vw(q), 0.0, A.add)
        mm(vw("pQ", 0, 128), vw("q16"), vw("I16"))
        if t:
            ts(vw("n1"), vw("pT", 256, 264), -16.0, A.mult, vw("c16"), A.add)
        else:
            mm(vw("pT", 264, 272), vw("on32"), vw("lim8"))
            copy(vw("limb"), vw("pT", 264, 272))
            ts(vw("n1"), vw("pT", 256, 264), -16.0, A.mult)
        ts(vw("n0"), vw("pT", 256, 264), 0.0, A.is_equal, -4194304.0, A.mult)
        tt(vw("n2"), vw("n1"), vw("limb"), A.add)
        tt(vw("thr"), vw("n2"), vw("n0"), A.add)
        if t:
            ts(vw("aa"), vw(v), 65535, A.bitwise_and)
            copy(vw("aF"), vw("aa"))
            mm(vw("pA", 0, 128), vw("aF"), vw("I32"))
        else:
            for m in range(16):
                mm(vw("pA", m, 128, 16), vw("CB", m, 2048, 16), vw("bo8b"))
        if t == VI - 1:
            sums()
        key = vw("pW", 0, 128)
        scan(vw("sm"), vw("d0s"), key, A.mult, A.add)
        scan(vw("mx"), vw("d0m"), key, A.add, A.max)
        tt(vw("stp"), vw("sm", 15, 128, 16), vw("thr"), A.is_ge)
        for w in range(8):
            ts(vw("oh", 16 * w, 16 * w + 16), vw("mx", 16 * w, 16 * w + 16), vw("mx", 16 * w + 15, 16 * w + 16), A.is_equal, vw("stp", w, w + 1), A.mult)
        scan(vw("pw"), vw("d0p"), vw("oh"), A.mult, A.max)
        for w in range(8):
            ts(vw("pr", 16 * w, 16 * w + 16), vw("pA", 16 * w, 16 * w + 16), vw("pw", 16 * w + 15, 16 * w + 16), A.mult)
        ts(vw("bb"), vw("pr"), 32768, A.bitwise_and)
        tt(vw("q2P"), vw("pQ", 0, 128), vw("bb"), A.subtract)
        mm(vw("pL", 384, 512), vw("q2P"), vw("I16"))
        copy(vw("q2u"), vw("pL", 384, 512))
        xgath("s", "x2", "q2u", 64, 128, True)
        ts(vw("e2"), vw("q2u"), 0, A.is_equal)
        xgath("v", "x2", "q2u", 0, 64, True)
        if t == 0:
            late_constants()
        mm(vw("pL", 0, 128), vw("e2"), vw("cm"))
        mm(vw("pL", 128, 256), vw("cm"), vw("e2"))
        scan(vw("bs", 0, 1024), vw("d0b", 0, 1024), vw("x2", 0, 1024), A.add, A.max)
        scan(vw("bs", 1024, 2048), vw("d0b", 1024, 2048), vw("x2", 1024, 2048), A.add, A.max)
        bl = vw("bs", 15, 2048, 16)
        ts(vw("lo"), bl, 0.0625, A.mult, 1280 - 0.46875, A.add)
        ku = vw("pU", 0, 128)
        mm(ku, vw("on", 0, 128, 1, 0, 1), vw("tie16", 0, 128, 1, 0, 1), True, False)
        mm(ku, vw("e2"), vw("bo256"), False, False)
        for m in range(16):
            mm(ku, vw("x2", m, 2048, 16), vw("I16b"), False, False)
        mm(ku, bl, vw("I16"), False, False)
        mm(ku, vw("lo"), vw("Im16"), False, True)
        ts(vw("eP"), vw("pL", 0, 128), -16.5, A.is_lt)
        ts(vw("eQ"), vw("pL", 128, 256), -16.5, A.is_lt)
        if t == VI - 1:
            tsixteenth()
        stopped()
        if t == 0:
            act(vw("aP0"), vw("pA", 0, 128))
        ts(vw("u1"), ku, 1.0 / 4096, A.mult, 1156.5 + 1.0 / 8192, A.add)
        mm(vw("pS", 128, 256), vw("u1"), vw("I16"))
        for j in range(16):
            act(vw("vf", j, 2048, 16), vw("pS", 128, 256), -1.0, 1279.0)
        scan(vw("mk"), vw("d0m"), ku, A.add, A.max)
        kk = vw("mk", 15, 128, 16)
        ts(vw("zi"), kk, 0.0625, A.mult, -0.46875, A.add)
        ts(vw("r16"), vw("zi"), 16.0, A.mult)
        for w in range(8):
            ts(vw("ok", 16 * w, 16 * w + 16), vw("m15"), vw("r16", w, w + 1), A.add, vw("mk", 16 * w + 15, 16 * w + 16), A.is_equal)
        tt(vw("pk"), vw("ok"), vw("pQ", 0, 128), A.mult)
        scan(vw("sk"), vw("d0s"), vw("pk"), A.mult, A.add)
        for w in range(8):
            ts(vw("AL", 16 * w, 16 * w + 16), vw("m16"), vw("sk", 16 * w + 15, 16 * w + 16), A.mult)
        mm(vw("pL", 256, 264), vw("AL"), vw("bo8h"))
        copy(vw("lk"), vw("pL", 256, 264))
        copy(vw("cd"), ind(vw("R"), vw("lk")))
        spread()
        mm(vw("pA", 256, 384), vw("ok"), vw("I16"))
        if t == 0:
            mm(vw("pA", 384, 512), vw("aP0"), vw("I32"))
        for a, b in ((0, 64), (64, 96), (96, 128)):
            d = vw("mn", 16 * a, 16 * b)
            tt(d, ind(vw("X", 16, 16 + D), vw("cd", a, b)), vw("vf", 16 * a, 16 * b), A.subtract)
            act(vw("xc", 16 * a, 16 * b), d, 1.0, 0.0, F.Abs)
            for j in range(16):
                mm(vw("pS", j, 128, 16, a, b), vw("xc", 16 * a + j, 16 * b, 16), vw("wm16"))
        if t == 0:
            tt(vw("aF"), vw("pA", 384, 512), vw("fil"), A.mult)
            ts(vw("w0"), vw("wy0"), 65536.0, A.mult)
            tt(vw("v0"), vw("aF"), vw("w0"), A.add)
        ts(vw("aM"), vw("aF"), vw("m64"), A.add)
        tt(vw("oka"), vw("pA", 256, 384), vw("aM"), A.mult)
        ts(vw("cd16"), vw("cd"), 16.0, A.add)
        ts(vw("fR"), vw("q2u"), 0, A.is_gt)
        tt(vw("vv"), vw(v), vw("fR"), A.mult)
        ts(vw("q2h"), vw("q2u"), 0.0, A.add)
        equal()
        mm(vw("pQ", 128, 256), vw("cd16"), vw("I16"))
        for w in range(8):
            mm(vw("pL", 272 + w, 273 + w), vw("eq", 128 * w, 128 * w + 128), vw("on", 0, 1))
        mm(vw("pA", 128, 256), vw("bo32"), vw("oka"), True, False)
        mm(vw("pA", 128, 256), vw("I32"), vw("bit"), False, True)

        def send(k):
            src = "%so%d" % (k, t + 1)
            lowd = T.cores[(rank + STRIDE[0]) % NR]
            hid = relay_of(core, T.cores[(rank + STRIDE[1]) % NR], topo)
            r1, p1 = topo.addr(lowd, core)
            r2, p2 = topo.addr(hid, core)
            tr = [RemoteDMATransfer(dst_ids=[DstId(rid=r1, pnc=p1)], dma_engine_mask=bits(topo, core, lowd, 8, False), remote_sem=T.sem["%sL%d" % (k, t + 1)],
                                    src=T[src][:, 0:H], dst=T["%s%d" % (k, t + 1)][:, 0:H]),
                  RemoteDMATransfer(dst_ids=[DstId(rid=r2, pnc=p2)], dma_engine_mask=bits(topo, core, hid, 8, True), remote_sem=T.sem["r%s%d" % (k, t + 1)],
                                    src=T[src][:, H:L], dst=T["r%s%d" % (k, t + 1)][:, :])]
            deps("g", [], [vw(src)])
            g.remote_dma_fused(tr, local_sem=T.sem["loc"])
            cnt["loc"] = cnt.get("loc", 0) + 16
        if t == VI - 1:
            dedupe()
            update()
            scatter()
            store(T.yx[:, :], vw("X", 16, 16 + D), "st0")
        tt(vw("ky"), vw("pS", 0, 128), vw("tief"), A.add)
        scan(vw("ms"), vw("d0m"), vw("ky"), A.add, A.max)
        for w in range(8):
            ts(vw("oj", 16 * w, 16 * w + 16), vw("ky", 16 * w, 16 * w + 16), vw("ms", 16 * w + 15, 16 * w + 16), A.is_equal)
        tt(vw("pn"), vw("oj"), vw("pQ", 128, 256), A.mult)
        scan(vw("sn"), vw("d0s"), vw("pn"), A.mult, A.add)
        for w in range(8):
            ts(vw("AN", 16 * w, 16 * w + 16), vw("eP", 16 * w, 16 * w + 16), vw("sn", 16 * w + 15, 16 * w + 16), A.mult)
        nq = vw("pL", 384, 512)
        mm(nq, vw("I16"), vw("q2h"), True, False)
        mm(nq, vw("AN"), vw("I16"), False, True)
        if t < VI - 1:
            copy(vw("qo%d" % (t + 1)), nq)
            send("q")
        else:
            ts(vw("yo"), nq, 0.0, A.is_equal, float(16 + D), A.mult)
            tt(vw("yo"), vw("yo"), nq, A.add)
            ts(vw("yt"), vw("yo"), -16.0, A.add)
            store(T.yp[:, :], vw("yt"), "st2")
        tt(vw("t3"), vw("pA", 128, 256), vw("eQ"), A.mult)
        tt(vw("vo%d" % (t + 1) if t < VI - 1 else "vI"), vw("vv"), vw("t3"), A.add)
        if t < VI - 1:
            send("v")
            sums()
            dedupe()
            stops()
            tsixteenth()
            update()
            scatter()
        else:
            ts(vw("bb"), vw("vI"), 16, A.arith_shift_right)
            copy(vw("yw"), vw("bb"))
            store(T.yq[:, :], vw("yw"), "st1")
    for s in SEMAPHORES:
        if cnt.get(s):
            g.wait_ge(T.sem[s], cnt[s])
